import numpy as np
import ml_dtypes


def mxq(x, axis, fmt="e4m3"):
    dtype, down = {"e4m3": (ml_dtypes.float8_e4m3fn, 7), "e5m2": (ml_dtypes.float8_e5m2, 14)}[fmt]
    v = np.moveaxis(np.asarray(x, np.float32).astype(ml_dtypes.bfloat16).astype(np.float64), axis, -1)
    blocks = v.reshape(v.shape[:-1] + (-1, 32))
    amax = np.abs(blocks).max(-1, keepdims=True)
    byte = np.maximum(np.where(amax > 0, np.frexp(amax)[1] - 1 + 127, 0) - down, 1)
    scale = np.exp2(byte - 127.0)
    codes = (blocks / scale).astype(np.float32).astype(dtype).astype(np.float64)
    return np.moveaxis((codes * scale).reshape(v.shape), -1, axis)


WIDE = False


def mx_kscale(k):
    if not WIDE:
        return np.ones(k)
    levels = np.array([10, -10, 5, -5, 0])
    if k % 512:
        return np.exp2(np.random.permutation(np.resize(levels, k // 32))).repeat(32)
    a = np.empty((k // 512, 16))
    for p in range(k // 512):
        a[p, :8] = np.random.permutation(np.resize(levels, 8))
        for g in range(8):
            far = levels[np.abs(levels - a[p, g]) >= 10]
            a[p, g + 8] = far[np.random.randint(len(far))]
    return np.exp2(a.ravel()).repeat(32)


def f64(x):
    return np.asarray(x).astype(np.float64)


def striped(idx):
    return np.tile(idx.reshape(-1, 16).T, (8, 1)).astype(np.uint16)


def unstriped(offs):
    return offs[:16].T.reshape(-1).astype(np.int64)


E2M1 = np.array([0.0, 0.5, 1.0, 1.5, 2.0, 3.0, 4.0, 6.0, -0.0, -0.5, -1.0, -1.5, -2.0, -3.0, -4.0, -6.0])


def pack_fp4(w):
    k, n = w.shape
    w = f64(np.asarray(w, np.float32).astype(ml_dtypes.bfloat16)).reshape(k // 32, 32, n)
    amax = np.abs(w).max(1)
    mant, ex = np.frexp(amax / 6.0)
    byte = np.clip(np.where(amax > 0, np.where(mant > 0.5, ex, ex - 1) + 127, 1), 1, 254)
    scaled = (w * np.exp2(127.0 - byte)[:, None, :]).reshape(k, n).astype(np.float32)
    c = np.ascontiguousarray(scaled.reshape(k // 512, 128, 4, n).transpose(0, 1, 3, 2)).astype(ml_dtypes.float4_e2m1fn).view(np.uint8) & 0xF
    words = (c[..., 0::2] | (c[..., 1::2] << 4)).reshape(k // 512, 128, 2 * n)
    return np.ascontiguousarray(words), np.ascontiguousarray(byte.astype(np.uint8).reshape(k // 512, 16, n))


def unpack_fp4(words, scales):
    g, _, n = scales.shape
    words = np.ascontiguousarray(words).reshape(g, 128, n, 2)
    nib = np.empty((g, 128, n, 4), np.uint8)
    nib[..., 0::2] = words & 0xF
    nib[..., 1::2] = words >> 4
    vals = E2M1[nib] * np.repeat(np.exp2(scales.astype(np.float64) - 127.0), 8, axis=1)[..., None]
    return vals.transpose(0, 1, 3, 2).reshape(g * 512, n)


def silu(v):
    return v / (1.0 + np.exp(-np.maximum(v, -700.0)))


K, T, S, D, H, N = 1024, 2048, 512, 3, 512, 128


def setup_inputs():
    n = np.random.standard_normal
    s = mx_kscale(K)[:, None]
    u = mx_kscale(H)
    packed_w2 = pack_fp4(n((H, N)) / np.sqrt(H) / u[:, None])
    return {
        "xT": (n((K, T)) * s).astype(np.float32),
        "w1": (n((K, H)) / np.sqrt(K) / s * u).astype(np.float32),
        "w2_words": packed_w2[0],
        "w2_scales": packed_w2[1],
        "taps": (n((H, D)) / np.sqrt(D)).astype(np.float32),
        "offs": striped(np.random.permutation(T)[:S]),
    }


def reference(xT, w1, w2_words, w2_scales, taps, offs):
    xq = mxq(f64(xT)[:, unstriped(offs)], 0, "e4m3")
    h = mxq(f64(w1), 0, "e4m3").T @ xq
    z = silu(f64(taps)[:, 0:1] * h + f64(taps)[:, 1:2] * (np.pad(h, ((0, 0), (1, 0)))[:, :S]) + f64(taps)[:, 2:3] * (np.pad(h, ((0, 0), (2, 0)))[:, :S]))
    return unpack_fp4(w2_words, w2_scales).T @ mxq(z, 0, "e4m3")

@@ -1,0 +1,177 @@
+from contextlib import ExitStack
+
+import concourse.mybir as mybir
+
+K, T, S, D, H, N = 1024, 2048, 512, 3, 512, 128
+FLOPS = 2 * K * H * S + 2 * H * N * S
+
+F32 = mybir.dt.float32
+BF16 = mybir.dt.bfloat16
+I32 = mybir.dt.int32
+U32 = mybir.dt.uint32
+U16 = mybir.dt.uint16
+U8 = mybir.dt.uint8
+FP8X4 = mybir.dt.float8_e4m3fn_x4
+FP4X4 = mybir.dt.float4_e2m1fn_x4
+MULT = mybir.AluOpType.mult
+ADD = mybir.AluOpType.add
+COPY = mybir.ActivationFunctionType.Copy
+SILU = mybir.ActivationFunctionType.Silu
+
+P = 128
+PACK = 4
+K_PASS = P * PACK
+HALF = S // 2
+CHUNKS = ((0, 256), (256, 128), (384, 128))
+W_HALF = H // 2
+M_HALF = W_HALF // PACK
+M_VECTOR = 44
+
+
+def tile_picked_dconv_silu_e_kernel(tc, xT, w1, w2_words, w2_scales, taps, offs, out):
+    nc = tc.nc
+    with ExitStack() as ctx:
+        keep = ctx.enter_context(tc.tile_pool(name="keep", bufs=1))
+        psum = ctx.enter_context(tc.psum_pool(name="psum", bufs=1))
+
+        offsets = keep.tile([P, S // 16], U16, name="offsets")
+        planes = [[keep.tile([P, T], F32, name=f"plane{g}{j}") for j in range(PACK)] for g in range(2)]
+        w_first = keep.tile([P, PACK, H], F32, name="w_first")
+        w_last = [keep.tile([P, PACK, W_HALF], F32, name=f"w_last{c}") for c in range(2)]
+
+        def load_plane(g, j):
+            rows = xT[g * K_PASS : (g + 1) * K_PASS, :].rearrange("(p j) t -> p j t", j=PACK)
+            nc.sync.dma_start(out=planes[g][j][:], in_=rows[:, j, :])
+
+        load_plane(0, 0)
+        nc.sync.dma_start(offsets[:], offs)
+        for j in range(1, PACK):
+            load_plane(0, j)
+        for j in range(PACK - 1):
+            load_plane(1, j)
+        nc.sync.dma_start(out=w_first[:], in_=w1[0:K_PASS, :].rearrange("(p j) c -> p j c", j=PACK))
+        load_plane(1, PACK - 1)
+        for c in range(2):
+            rows = w1[K_PASS:K, :].rearrange("(p j) c -> p j c", j=PACK)
+            nc.sync.dma_start(out=w_last[c][:], in_=rows[:, :, c * W_HALF : (c + 1) * W_HALF])
+
+        tap = keep.tile([P, PACK, D], F32, name="tap")
+        w2_codes = keep.tile([P, 2 * N], U8, name="w2_codes", align_bytes=64)
+        w2_plane = keep.tile([P, N], U8, name="w2_plane", align_bytes=64)
+        zeros = keep.tile([P, PACK, D - 1], F32, name="zeros")
+        nc.gpsimd.memset(zeros[:], 0.0)
+        nc.gpsimd.memset(w2_plane[:], 0)
+        nc.gpsimd.dma_start(out=tap[:], in_=taps.rearrange("(p t) d -> p t d", t=PACK))
+        nc.gpsimd.dma_start(out=w2_codes[:].bitcast(I32), in_=w2_words[0].bitcast(I32))
+        for q in range(4):
+            nc.gpsimd.dma_start(
+                out=w2_plane[32 * q : 32 * q + 4, :].bitcast(I32), in_=w2_scales[0, 4 * q : 4 * q + 4, :].bitcast(I32)
+            )
+
+        acc = keep.tile([P, PACK, S + 8], F32, name="acc")
+        nc.scalar.activation(acc[:, :, 0 : D - 1], zeros[:], SILU)
+
+        picked = [keep.tile([P, S, PACK], BF16, name=f"picked{g}", align_bytes=64) for g in range(2)]
+        x_codes = [keep.tile([P, S], U32, name=f"x_codes{g}", align_bytes=64) for g in range(2)]
+        x_plane = [keep.tile([P, S], U8, name=f"x_plane{g}", align_bytes=64) for g in range(2)]
+        dealt = [keep.tile([P, PACK, P, PACK], BF16, name=f"dealt{g}", align_bytes=64) for g in range(2)]
+        w_codes = [keep.tile([P, H], U32, name=f"w_codes{g}", align_bytes=64) for g in range(2)]
+        w_plane = [keep.tile([P, H], U8, name=f"w_plane{g}", align_bytes=64) for g in range(2)]
+        hidden = [[psum.tile([P, HALF], F32, name=f"hidden{h}{t}", tag=f"bank{h}{t}") for t in range(PACK)] for h in range(2)]
+
+        def gather(g, j):
+            nc.vector.tensor_copy(picked[g][:, :, j], planes[g][j][:].indirect(offsets[:]))
+
+        def quantize_x(g):
+            nc.vector.quantize_mx(x_codes[g][:].bitcast(FP8X4), x_plane[g][:], picked[g][:].rearrange("p s j -> p (s j)"))
+
+        def deal(copy, g, raw, m_raw, m_count, m_dealt):
+            src = raw[:].rearrange("p j (m t) -> p m j t", t=PACK)[:, m_raw : m_raw + m_count]
+            dst = dealt[g][:].rearrange("p t m j -> p m j t")[:, m_dealt : m_dealt + m_count]
+            copy(dst, src)
+
+        def project(g, h, t):
+            cols = slice(t * P, (t + 1) * P)
+            toks = slice(h * HALF, (h + 1) * HALF)
+            nc.tensor.matmul_mx(
+                hidden[h][t][:], w_codes[g][:, cols].bitcast(FP8X4), w_plane[g][:, cols],
+                x_codes[g][:, toks].bitcast(FP8X4), x_plane[g][:, toks], start=(g == 0), stop=(g == 1),
+            )
+
+        for j in range(PACK):
+            gather(0, j)
+        quantize_x(0)
+        for j in range(PACK - 1):
+            gather(1, j)
+        deal(nc.scalar.copy, 0, w_first, 0, P, 0)
+        nc.vector.quantize_mx(w_codes[0][:].bitcast(FP8X4), w_plane[0][:], dealt[0][:].rearrange("p t m j -> p (t m j)"))
+        for h in range(2):
+            for t in range(PACK):
+                project(0, h, t)
+        gather(1, PACK - 1)
+        quantize_x(1)
+        deal(nc.scalar.copy, 1, w_last[0], 0, M_HALF, 0)
+        deal(nc.vector.tensor_copy, 1, w_last[1], 0, M_VECTOR, M_HALF)
+        deal(nc.scalar.copy, 1, w_last[1], M_VECTOR, M_HALF - M_VECTOR, M_HALF + M_VECTOR)
+        for t in range(PACK):
+            cols = slice(t * P, (t + 1) * P)
+            nc.vector.quantize_mx(w_codes[1][:, cols].bitcast(FP8X4), w_plane[1][:, cols], dealt[1][:, t].rearrange("p m j -> p (m j)"))
+        for h in range(2):
+            for t in range(PACK):
+                project(1, h, t)
+
+        for h in range(2):
+            for t in range(PACK):
+                nc.scalar.activation(acc[:, t, h * HALF + 2 : (h + 1) * HALF + 2], hidden[h][t][:], COPY, scale=tap[:, t, 2:3])
+
+        summed = [keep.tile([P, PACK, n], F32, name=f"summed{s}") for s, n in CHUNKS]
+        z = [keep.tile([P, n, PACK], BF16, name=f"z{s}", align_bytes=64) for s, n in CHUNKS]
+        z_codes = [keep.tile([P, n], U32, name=f"z_codes{s}", align_bytes=64) for s, n in CHUNKS]
+        z_plane = [keep.tile([P, n], U8, name=f"z_plane{s}", align_bytes=64) for s, n in CHUNKS]
+        result = [keep.tile([P, n], F32, name=f"result{s}") for s, n in CHUNKS]
+
+        def bank_cols(c, t):
+            s, n = CHUNKS[c]
+            return hidden[s // HALF][t][:, s % HALF : s % HALF + n]
+
+        def add_tap1(c, t):
+            s, n = CHUNKS[c]
+            window = acc[:, t, s + 1 : s + n + 1]
+            nc.vector.scalar_tensor_tensor(window, bank_cols(c, t), tap[:, t, 1:2], window, MULT, ADD)
+
+        def add_tap0(c, t):
+            s, n = CHUNKS[c]
+            nc.vector.scalar_tensor_tensor(summed[c][:, t, :], bank_cols(c, t), tap[:, t, 0:1], acc[:, t, s : s + n], MULT, ADD)
+
+        def convolve(c):
+            add_tap1(c, 0)
+            for t in range(1, PACK):
+                add_tap1(c, t)
+                add_tap0(c, t - 1)
+            add_tap0(c, PACK - 1)
+
+        def activate(c):
+            nc.scalar.activation(
+                z[c][:].rearrange("p (s i) t -> p s t i", i=4), summed[c][:].rearrange("p t (s i) -> p s t i", i=4), SILU
+            )
+
+        def finish(c, copy):
+            s, n = CHUNKS[c]
+            nc.vector.quantize_mx(z_codes[c][:].bitcast(FP8X4), z_plane[c][:], z[c][:].rearrange("p s t -> p (s t)"))
+            product = psum.tile([P, HALF], F32, name=f"product{c}", tag=f"bank0{c}")
+            nc.tensor.matmul_mx(
+                product[:, 0:n], w2_codes[:].bitcast(FP4X4), w2_plane[:], z_codes[c][:].bitcast(FP8X4), z_plane[c][:],
+                start=True, stop=True,
+            )
+            copy(result[c][:], product[:, 0:n])
+            nc.sync.dma_start(out=out[:, s : s + n], in_=result[c][:])
+
+        convolve(0)
+        activate(0)
+        convolve(1)
+        activate(1)
+        finish(0, nc.scalar.copy)
+        convolve(2)
+        activate(2)
+        finish(1, nc.scalar.copy)
+        finish(2, nc.vector.tensor_copy)

@@ -26,6 +26,7 @@ CHUNKS = ((0, 256), (256, 128), (384, 128))
 W_HALF = H // 2
 M_HALF = W_HALF // PACK
 M_VECTOR = 44
+M_VECTOR_FIRST = 80
 
 
 def tile_picked_dconv_silu_e_kernel(tc, xT, w1, w2_words, w2_scales, taps, offs, out):
@@ -35,36 +36,37 @@ def tile_picked_dconv_silu_e_kernel(tc, xT, w1, w2_words, w2_scales, taps, offs,
         psum = ctx.enter_context(tc.psum_pool(name="psum", bufs=1))
 
         offsets = keep.tile([P, S // 16], U16, name="offsets")
-        planes = [[keep.tile([P, T], F32, name=f"plane{g}{j}") for j in range(PACK)] for g in range(2)]
         w_first = keep.tile([P, PACK, H], F32, name="w_first")
         w_last = [keep.tile([P, PACK, W_HALF], F32, name=f"w_last{c}") for c in range(2)]
-
-        def load_plane(g, j):
-            rows = xT[g * K_PASS : (g + 1) * K_PASS, :].rearrange("(p j) t -> p j t", j=PACK)
-            nc.sync.dma_start(out=planes[g][j][:], in_=rows[:, j, :])
-
-        load_plane(0, 0)
-        nc.sync.dma_start(offsets[:], offs)
-        for j in range(1, PACK):
-            load_plane(0, j)
-        for j in range(PACK - 1):
-            load_plane(1, j)
-        nc.sync.dma_start(out=w_first[:], in_=w1[0:K_PASS, :].rearrange("(p j) c -> p j c", j=PACK))
-        load_plane(1, PACK - 1)
-        for c in range(2):
-            rows = w1[K_PASS:K, :].rearrange("(p j) c -> p j c", j=PACK)
-            nc.sync.dma_start(out=w_last[c][:], in_=rows[:, :, c * W_HALF : (c + 1) * W_HALF])
-
         tap = keep.tile([P, PACK, D], F32, name="tap")
         w2_codes = keep.tile([P, 2 * N], U8, name="w2_codes", align_bytes=64)
         w2_plane = keep.tile([P, N], U8, name="w2_plane", align_bytes=64)
         zeros = keep.tile([P, PACK, D - 1], F32, name="zeros")
         nc.gpsimd.memset(zeros[:], 0.0)
         nc.gpsimd.memset(w2_plane[:], 0)
-        nc.gpsimd.dma_start(out=tap[:], in_=taps.rearrange("(p t) d -> p t d", t=PACK))
-        nc.gpsimd.dma_start(out=w2_codes[:].bitcast(I32), in_=w2_words[0].bitcast(I32))
+        planes = {}
+
+        def load_planes(g, j, count):
+            rows = xT[g * K_PASS : (g + 1) * K_PASS, :].rearrange("(p j) t -> p j t", j=PACK)
+            loaded = keep.tile([P, count, T], F32, name=f"planes{g}{j}")
+            nc.sync.dma_start(out=loaded[:], in_=rows[:, j : j + count, :])
+            for i in range(count):
+                planes[g, j + i] = loaded[:, i, :]
+
+        load_planes(0, 0, 2)
+        nc.sync.dma_start(offsets[:], offs)
+        load_planes(0, 2, 2)
+        load_planes(1, 0, 2)
+        load_planes(1, 2, 1)
+        nc.sync.dma_start(out=w_first[:], in_=w1[0:K_PASS, :].rearrange("(p j) c -> p j c", j=PACK))
+        load_planes(1, 3, 1)
+        for c in range(2):
+            rows = w1[K_PASS:K, :].rearrange("(p j) c -> p j c", j=PACK)
+            nc.sync.dma_start(out=w_last[c][:], in_=rows[:, :, c * W_HALF : (c + 1) * W_HALF])
+        nc.sync.dma_start(out=tap[:], in_=taps.rearrange("(p t) d -> p t d", t=PACK))
+        nc.sync.dma_start(out=w2_codes[:].bitcast(I32), in_=w2_words[0].bitcast(I32))
         for q in range(4):
-            nc.gpsimd.dma_start(
+            nc.sync.dma_start(
                 out=w2_plane[32 * q : 32 * q + 4, :].bitcast(I32), in_=w2_scales[0, 4 * q : 4 * q + 4, :].bitcast(I32)
             )
 
@@ -79,11 +81,14 @@ def tile_picked_dconv_silu_e_kernel(tc, xT, w1, w2_words, w2_scales, taps, offs,
         w_plane = [keep.tile([P, H], U8, name=f"w_plane{g}", align_bytes=64) for g in range(2)]
         hidden = [[psum.tile([P, HALF], F32, name=f"hidden{h}{t}", tag=f"bank{h}{t}") for t in range(PACK)] for h in range(2)]
 
-        def gather(g, j):
-            nc.vector.tensor_copy(picked[g][:, :, j], planes[g][j][:].indirect(offsets[:]))
+        def gather(g, j, s, n):
+            nc.vector.tensor_copy(picked[g][:, s : s + n, j], planes[g, j].indirect(offsets[:, s // 16 : (s + n) // 16]))
 
-        def quantize_x(g):
-            nc.vector.quantize_mx(x_codes[g][:].bitcast(FP8X4), x_plane[g][:], picked[g][:].rearrange("p s j -> p (s j)"))
+        def quantize_x(g, s, n):
+            nc.vector.quantize_mx(
+                x_codes[g][:, s : s + n].bitcast(FP8X4), x_plane[g][:, s : s + n],
+                picked[g][:, s : s + n, :].rearrange("p s j -> p (s j)"),
+            )
 
         def deal(copy, g, raw, m_raw, m_count, m_dealt):
             src = raw[:].rearrange("p j (m t) -> p m j t", t=PACK)[:, m_raw : m_raw + m_count]
@@ -99,17 +104,20 @@ def tile_picked_dconv_silu_e_kernel(tc, xT, w1, w2_words, w2_scales, taps, offs,
             )
 
         for j in range(PACK):
-            gather(0, j)
-        quantize_x(0)
+            gather(0, j, 0, S)
+        quantize_x(0, 0, S)
         for j in range(PACK - 1):
-            gather(1, j)
-        deal(nc.scalar.copy, 0, w_first, 0, P, 0)
+            gather(1, j, 0, S)
+        deal(nc.vector.tensor_copy, 0, w_first, 0, M_VECTOR_FIRST, 0)
+        deal(nc.scalar.copy, 0, w_first, M_VECTOR_FIRST, P - M_VECTOR_FIRST, M_VECTOR_FIRST)
         nc.vector.quantize_mx(w_codes[0][:].bitcast(FP8X4), w_plane[0][:], dealt[0][:].rearrange("p t m j -> p (t m j)"))
         for h in range(2):
             for t in range(PACK):
                 project(0, h, t)
-        gather(1, PACK - 1)
-        quantize_x(1)
+        for h in range(2):
+            gather(1, PACK - 1, h * HALF, HALF)
+        for h in range(2):
+            quantize_x(1, h * HALF, HALF)
         deal(nc.scalar.copy, 1, w_last[0], 0, M_HALF, 0)
         deal(nc.vector.tensor_copy, 1, w_last[1], 0, M_VECTOR, M_HALF)
         deal(nc.scalar.copy, 1, w_last[1], M_VECTOR, M_HALF - M_VECTOR, M_HALF + M_VECTOR)
@@ -128,50 +136,46 @@ def tile_picked_dconv_silu_e_kernel(tc, xT, w1, w2_words, w2_scales, taps, offs,
         z = [keep.tile([P, n, PACK], BF16, name=f"z{s}", align_bytes=64) for s, n in CHUNKS]
         z_codes = [keep.tile([P, n], U32, name=f"z_codes{s}", align_bytes=64) for s, n in CHUNKS]
         z_plane = [keep.tile([P, n], U8, name=f"z_plane{s}", align_bytes=64) for s, n in CHUNKS]
-        result = [keep.tile([P, n], F32, name=f"result{s}") for s, n in CHUNKS]
 
-        def bank_cols(c, t):
-            s, n = CHUNKS[c]
-            return hidden[s // HALF][t][:, s % HALF : s % HALF + n]
-
-        def add_tap1(c, t):
-            s, n = CHUNKS[c]
-            window = acc[:, t, s + 1 : s + n + 1]
-            nc.vector.scalar_tensor_tensor(window, bank_cols(c, t), tap[:, t, 1:2], window, MULT, ADD)
+        def add_tap1(h, t):
+            window = acc[:, t, h * HALF + 1 : (h + 1) * HALF + 1]
+            nc.vector.scalar_tensor_tensor(window, hidden[h][t][:], tap[:, t, 1:2], window, MULT, ADD)
 
         def add_tap0(c, t):
             s, n = CHUNKS[c]
-            nc.vector.scalar_tensor_tensor(summed[c][:, t, :], bank_cols(c, t), tap[:, t, 0:1], acc[:, t, s : s + n], MULT, ADD)
-
-        def convolve(c):
-            add_tap1(c, 0)
-            for t in range(1, PACK):
-                add_tap1(c, t)
-                add_tap0(c, t - 1)
-            add_tap0(c, PACK - 1)
+            bank = hidden[s // HALF][t][:, s % HALF : s % HALF + n]
+            nc.vector.scalar_tensor_tensor(summed[c][:, t, :], bank, tap[:, t, 0:1], acc[:, t, s : s + n], MULT, ADD)
 
         def activate(c):
             nc.scalar.activation(
                 z[c][:].rearrange("p (s i) t -> p s t i", i=4), summed[c][:].rearrange("p t (s i) -> p s t i", i=4), SILU
             )
 
-        def finish(c, copy):
-            s, n = CHUNKS[c]
+        def multiply(c, product):
             nc.vector.quantize_mx(z_codes[c][:].bitcast(FP8X4), z_plane[c][:], z[c][:].rearrange("p s t -> p (s t)"))
-            product = psum.tile([P, HALF], F32, name=f"product{c}", tag=f"bank0{c}")
             nc.tensor.matmul_mx(
-                product[:, 0:n], w2_codes[:].bitcast(FP4X4), w2_plane[:], z_codes[c][:].bitcast(FP8X4), z_plane[c][:],
+                product, w2_codes[:].bitcast(FP4X4), w2_plane[:], z_codes[c][:].bitcast(FP8X4), z_plane[c][:],
                 start=True, stop=True,
             )
-            copy(result[c][:], product[:, 0:n])
-            nc.sync.dma_start(out=out[:, s : s + n], in_=result[c][:])
 
-        convolve(0)
+        add_tap1(0, 0)
+        for t in range(1, PACK):
+            add_tap1(0, t)
+            add_tap0(0, t - 1)
+        add_tap0(0, PACK - 1)
         activate(0)
-        convolve(1)
-        activate(1)
-        finish(0, nc.scalar.copy)
-        convolve(2)
-        activate(2)
-        finish(1, nc.scalar.copy)
-        finish(2, nc.vector.tensor_copy)
+        for t in range(PACK):
+            add_tap1(1, t)
+        for c in (1, 2):
+            for t in range(PACK):
+                add_tap0(c, t)
+            activate(c)
+
+        products = [psum.tile([P, n], F32, name=f"product{c}", tag=f"bank0{c}") for c, (s, n) in enumerate(CHUNKS)]
+        results = [keep.tile([P, n], F32, name=f"result{s}") for s, n in CHUNKS]
+        for c in range(3):
+            multiply(c, products[c][:])
+        for c, copy, queue in ((0, nc.scalar.copy, nc.sync), (1, nc.scalar.copy, nc.sync), (2, nc.vector.tensor_copy, nc.scalar)):
+            s, n = CHUNKS[c]
+            copy(results[c][:], products[c][:])
+            queue.dma_start(out=out[:, s : s + n], in_=results[c][:])

@@ -53,11 +53,12 @@ def tile_picked_dconv_silu_e_kernel(tc, xT, w1, w2_words, w2_scales, taps, offs,
             for i in range(count):
                 planes[g, j + i] = loaded[:, i, :]
 
-        load_planes(0, 0, 2)
+        load_planes(0, 0, 1)
         nc.sync.dma_start(offsets[:], offs)
-        load_planes(0, 2, 2)
-        load_planes(1, 0, 2)
-        load_planes(1, 2, 1)
+        for j in range(1, PACK):
+            load_planes(0, j, 1)
+        for j in range(PACK - 1):
+            load_planes(1, j, 1)
         nc.sync.dma_start(out=w_first[:], in_=w1[0:K_PASS, :].rearrange("(p j) c -> p j c", j=PACK))
         load_planes(1, 3, 1)
         for c in range(2):
@@ -90,9 +91,9 @@ def tile_picked_dconv_silu_e_kernel(tc, xT, w1, w2_words, w2_scales, taps, offs,
                 picked[g][:, s : s + n, :].rearrange("p s j -> p (s j)"),
             )
 
-        def deal(copy, g, raw, m_raw, m_count, m_dealt):
-            src = raw[:].rearrange("p j (m t) -> p m j t", t=PACK)[:, m_raw : m_raw + m_count]
-            dst = dealt[g][:].rearrange("p t m j -> p m j t")[:, m_dealt : m_dealt + m_count]
+        def deal(copy, g, raw, m_raw, m_count, m_dealt, slots=slice(0, PACK)):
+            src = raw[:].rearrange("p j (m t) -> p m j t", t=PACK)[:, m_raw : m_raw + m_count, :, slots]
+            dst = dealt[g][:].rearrange("p t m j -> p m j t")[:, m_dealt : m_dealt + m_count, :, slots]
             copy(dst, src)
 
         def project(g, h, t):
@@ -119,8 +120,9 @@ def tile_picked_dconv_silu_e_kernel(tc, xT, w1, w2_words, w2_scales, taps, offs,
         for h in range(2):
             quantize_x(1, h * HALF, HALF)
         deal(nc.scalar.copy, 1, w_last[0], 0, M_HALF, 0)
-        deal(nc.vector.tensor_copy, 1, w_last[1], 0, M_VECTOR, M_HALF)
-        deal(nc.scalar.copy, 1, w_last[1], M_VECTOR, M_HALF - M_VECTOR, M_HALF + M_VECTOR)
+        for slots in (slice(0, 2), slice(2, 4)):
+            deal(nc.vector.tensor_copy, 1, w_last[1], 0, M_VECTOR, M_HALF, slots)
+            deal(nc.scalar.copy, 1, w_last[1], M_VECTOR, M_HALF - M_VECTOR, M_HALF + M_VECTOR, slots)
         for t in range(PACK):
             cols = slice(t * P, (t + 1) * P)
             nc.vector.quantize_mx(w_codes[1][:, cols].bitcast(FP8X4), w_plane[1][:, cols], dealt[1][:, t].rearrange("p m j -> p (m j)"))

@@ -37,7 +37,7 @@ def tile_picked_dconv_silu_e_kernel(tc, xT, w1, w2_words, w2_scales, taps, offs,
 
         offsets = keep.tile([P, S // 16], U16, name="offsets")
         w_first = keep.tile([P, PACK, H], F32, name="w_first")
-        w_last = [keep.tile([P, PACK, W_HALF], F32, name=f"w_last{c}") for c in range(2)]
+        w_last = [keep.tile([P, PACK, W_HALF], F32, name=f"w_last{c}", tag=f"w_last{c}", align_bytes=64) for c in range(2)]
         tap = keep.tile([P, PACK, D], F32, name="tap")
         w2_codes = keep.tile([P, 2 * N], U8, name="w2_codes", align_bytes=64)
         w2_plane = keep.tile([P, N], U8, name="w2_plane", align_bytes=64)
@@ -75,8 +75,8 @@ def tile_picked_dconv_silu_e_kernel(tc, xT, w1, w2_words, w2_scales, taps, offs,
         nc.scalar.activation(acc[:, :, 0 : D - 1], zeros[:], SILU)
 
         picked = [keep.tile([P, S, PACK], BF16, name=f"picked{g}", align_bytes=64) for g in range(2)]
-        x_codes = [keep.tile([P, S], U32, name=f"x_codes{g}", align_bytes=64) for g in range(2)]
-        x_plane = [keep.tile([P, S], U8, name=f"x_plane{g}", align_bytes=64) for g in range(2)]
+        x_codes = {}
+        x_plane = {(g, h): keep.tile([P, HALF], U8, name=f"x_plane{g}{h}", align_bytes=64) for g in range(2) for h in range(2)}
         dealt = [keep.tile([P, PACK, P, PACK], BF16, name=f"dealt{g}", align_bytes=64) for g in range(2)]
         w_codes = [keep.tile([P, H], U32, name=f"w_codes{g}", align_bytes=64) for g in range(2)]
         w_plane = [keep.tile([P, H], U8, name=f"w_plane{g}", align_bytes=64) for g in range(2)]
@@ -85,10 +85,11 @@ def tile_picked_dconv_silu_e_kernel(tc, xT, w1, w2_words, w2_scales, taps, offs,
         def gather(g, j, s, n):
             nc.vector.tensor_copy(picked[g][:, s : s + n, j], planes[g, j].indirect(offsets[:, s // 16 : (s + n) // 16]))
 
-        def quantize_x(g, s, n):
+        def quantize_x(g, h, tag):
+            x_codes[g, h] = keep.tile([P, HALF], U32, name=f"x_codes{g}{h}", tag=tag, align_bytes=64)
             nc.vector.quantize_mx(
-                x_codes[g][:, s : s + n].bitcast(FP8X4), x_plane[g][:, s : s + n],
-                picked[g][:, s : s + n, :].rearrange("p s j -> p (s j)"),
+                x_codes[g, h][:].bitcast(FP8X4), x_plane[g, h][:],
+                picked[g][:, h * HALF : (h + 1) * HALF, :].rearrange("p s j -> p (s j)"),
             )
 
         def deal(copy, g, raw, m_raw, m_count, m_dealt, slots=slice(0, PACK)):
@@ -98,15 +99,15 @@ def tile_picked_dconv_silu_e_kernel(tc, xT, w1, w2_words, w2_scales, taps, offs,
 
         def project(g, h, t):
             cols = slice(t * P, (t + 1) * P)
-            toks = slice(h * HALF, (h + 1) * HALF)
             nc.tensor.matmul_mx(
                 hidden[h][t][:], w_codes[g][:, cols].bitcast(FP8X4), w_plane[g][:, cols],
-                x_codes[g][:, toks].bitcast(FP8X4), x_plane[g][:, toks], start=(g == 0), stop=(g == 1),
+                x_codes[g, h][:].bitcast(FP8X4), x_plane[g, h][:], start=(g == 0), stop=(g == 1),
             )
 
         for j in range(PACK):
             gather(0, j, 0, S)
-        quantize_x(0, 0, S)
+        for h in range(2):
+            quantize_x(0, h, f"x_codes0{h}")
         for j in range(PACK - 1):
             gather(1, j, 0, S)
         deal(nc.vector.tensor_copy, 0, w_first, 0, M_VECTOR_FIRST, 0)
@@ -117,8 +118,7 @@ def tile_picked_dconv_silu_e_kernel(tc, xT, w1, w2_words, w2_scales, taps, offs,
                 project(0, h, t)
         for h in range(2):
             gather(1, PACK - 1, h * HALF, HALF)
-        for h in range(2):
-            quantize_x(1, h * HALF, HALF)
+        quantize_x(1, 0, "x_codes10")
         deal(nc.scalar.copy, 1, w_last[0], 0, M_HALF, 0)
         for slots in (slice(0, 2), slice(2, 4)):
             deal(nc.vector.tensor_copy, 1, w_last[1], 0, M_VECTOR, M_HALF, slots)
@@ -126,6 +126,7 @@ def tile_picked_dconv_silu_e_kernel(tc, xT, w1, w2_words, w2_scales, taps, offs,
         for t in range(PACK):
             cols = slice(t * P, (t + 1) * P)
             nc.vector.quantize_mx(w_codes[1][:, cols].bitcast(FP8X4), w_plane[1][:, cols], dealt[1][:, t].rearrange("p m j -> p (m j)"))
+        quantize_x(1, 1, "w_last1")
         for h in range(2):
             for t in range(PACK):
                 project(1, h, t)

@@ -22,7 +22,10 @@ P = 128
 PACK = 4
 K_PASS = P * PACK
 HALF = S // 2
-CHUNKS = ((0, 256), (256, 128), (384, 128))
+ACT_PIECES = ((0, 128), (128, 128), (256, 128), (384, 64), (448, 64))
+OUT_PIECES = ((0, 256), (256, 128), (384, 128))
+GPSIMD_SLOTS = (3,)
+SECOND_ORDER = (3, 2, 1, 0)
 W_HALF = H // 2
 M_HALF = W_HALF // PACK
 M_VECTOR = 44
@@ -110,9 +113,15 @@ def tile_picked_dconv_silu_e_kernel(tc, xT, w1, w2_words, w2_scales, taps, offs,
             quantize_x(0, h, f"x_codes0{h}")
         for j in range(PACK - 1):
             gather(1, j, 0, S)
-        deal(nc.vector.tensor_copy, 0, w_first, 0, M_VECTOR_FIRST, 0)
-        deal(nc.scalar.copy, 0, w_first, M_VECTOR_FIRST, P - M_VECTOR_FIRST, M_VECTOR_FIRST)
-        nc.vector.quantize_mx(w_codes[0][:].bitcast(FP8X4), w_plane[0][:], dealt[0][:].rearrange("p t m j -> p (t m j)"))
+        for slots in (slice(0, 2), slice(2, 4)):
+            deal(nc.vector.tensor_copy, 0, w_first, 0, M_VECTOR_FIRST, 0, slots)
+            deal(nc.scalar.copy, 0, w_first, M_VECTOR_FIRST, P - M_VECTOR_FIRST, M_VECTOR_FIRST, slots)
+        for pair in range(2):
+            cols = slice(pair * 2 * P, (pair + 1) * 2 * P)
+            nc.vector.quantize_mx(
+                w_codes[0][:, cols].bitcast(FP8X4), w_plane[0][:, cols],
+                dealt[0][:, 2 * pair : 2 * pair + 2].rearrange("p t m j -> p (t m j)"),
+            )
         for h in range(2):
             for t in range(PACK):
                 project(0, h, t)
@@ -127,58 +136,78 @@ def tile_picked_dconv_silu_e_kernel(tc, xT, w1, w2_words, w2_scales, taps, offs,
             cols = slice(t * P, (t + 1) * P)
             nc.vector.quantize_mx(w_codes[1][:, cols].bitcast(FP8X4), w_plane[1][:, cols], dealt[1][:, t].rearrange("p m j -> p (m j)"))
         quantize_x(1, 1, "w_last1")
-        for h in range(2):
-            for t in range(PACK):
-                project(1, h, t)
+        for t in range(PACK):
+            project(1, 0, t)
+        for t in SECOND_ORDER:
+            project(1, 1, t)
 
-        for h in range(2):
-            for t in range(PACK):
-                nc.scalar.activation(acc[:, t, h * HALF + 2 : (h + 1) * HALF + 2], hidden[h][t][:], COPY, scale=tap[:, t, 2:3])
+        plain = {t: keep.tile([P, HALF + 8], F32, name=f"plain{t}") for t in GPSIMD_SLOTS}
+        older = {t: keep.tile([P, HALF], F32, name=f"older{t}") for t in GPSIMD_SLOTS}
+        for t in range(PACK):
+            n = HALF - 2 if t in GPSIMD_SLOTS else HALF
+            nc.scalar.activation(acc[:, t, 2 : n + 2], hidden[0][t][:, :n], COPY, scale=tap[:, t, 2:3])
+            if t in GPSIMD_SLOTS:
+                nc.scalar.copy(plain[t][:, 0:2], hidden[0][t][:, n:])
+        for t in SECOND_ORDER:
+            if t in GPSIMD_SLOTS:
+                scaled = keep.tile([P, HALF], F32, name=f"scaled{t}")
+                nc.scalar.copy(plain[t][:, 2 : HALF + 1], hidden[1][t][:, : HALF - 1])
+                nc.gpsimd.tensor_scalar(older[t][:], plain[t][:, 0:HALF], tap[:, t, 2:3], 0.0, MULT, ADD)
+                nc.gpsimd.tensor_scalar(scaled[:], plain[t][:, 1 : HALF + 1], tap[:, t, 1:2], 0.0, MULT, ADD)
+                nc.gpsimd.tensor_tensor(older[t][:], older[t][:], scaled[:], ADD)
+            else:
+                nc.scalar.activation(acc[:, t, HALF + 2 : S + 2], hidden[1][t][:], COPY, scale=tap[:, t, 2:3])
 
-        summed = [keep.tile([P, PACK, n], F32, name=f"summed{s}") for s, n in CHUNKS]
-        z = [keep.tile([P, n, PACK], BF16, name=f"z{s}", align_bytes=64) for s, n in CHUNKS]
-        z_codes = [keep.tile([P, n], U32, name=f"z_codes{s}", align_bytes=64) for s, n in CHUNKS]
-        z_plane = [keep.tile([P, n], U8, name=f"z_plane{s}", align_bytes=64) for s, n in CHUNKS]
+        pieces = dict(ACT_PIECES)
+        summed = {s: keep.tile([P, PACK, n], F32, name=f"summed{s}") for s, n in ACT_PIECES}
+        z = {s: keep.tile([P, n, PACK], BF16, name=f"z{s}", align_bytes=64) for s, n in ACT_PIECES}
+        z_codes = [keep.tile([P, n], U32, name=f"z_codes{s}", align_bytes=64) for s, n in OUT_PIECES]
+        z_plane = [keep.tile([P, n], U8, name=f"z_plane{s}", align_bytes=64) for s, n in OUT_PIECES]
 
         def add_tap1(h, t):
-            window = acc[:, t, h * HALF + 1 : (h + 1) * HALF + 1]
-            nc.vector.scalar_tensor_tensor(window, hidden[h][t][:], tap[:, t, 1:2], window, MULT, ADD)
+            n = HALF - 1 if t in GPSIMD_SLOTS else HALF
+            window = acc[:, t, h * HALF + 1 : h * HALF + n + 1]
+            nc.vector.scalar_tensor_tensor(window, hidden[h][t][:, :n], tap[:, t, 1:2], window, MULT, ADD)
 
-        def add_tap0(c, t):
-            s, n = CHUNKS[c]
+        def add_tap0(s, t):
+            n = pieces[s]
             bank = hidden[s // HALF][t][:, s % HALF : s % HALF + n]
-            nc.vector.scalar_tensor_tensor(summed[c][:, t, :], bank, tap[:, t, 0:1], acc[:, t, s : s + n], MULT, ADD)
+            before = older[t][:, s - HALF : s - HALF + n] if t in GPSIMD_SLOTS and s >= HALF else acc[:, t, s : s + n]
+            nc.vector.scalar_tensor_tensor(summed[s][:, t, :], bank, tap[:, t, 0:1], before, MULT, ADD)
 
-        def activate(c):
+        def activate(s):
             nc.scalar.activation(
-                z[c][:].rearrange("p (s i) t -> p s t i", i=4), summed[c][:].rearrange("p t (s i) -> p s t i", i=4), SILU
+                z[s][:].rearrange("p (s i) t -> p s t i", i=4), summed[s][:].rearrange("p t (s i) -> p s t i", i=4), SILU
             )
 
-        def multiply(c, product):
-            nc.vector.quantize_mx(z_codes[c][:].bitcast(FP8X4), z_plane[c][:], z[c][:].rearrange("p s t -> p (s t)"))
+        for h in range(2):
+            order = [t for t in (range(PACK), SECOND_ORDER)[h] if h == 0 or t not in GPSIMD_SLOTS]
+            add_tap1(h, order[0])
+            for before, t in zip(order, order[1:]):
+                add_tap1(h, t)
+                add_tap0(h * HALF, before)
+            for t in range(PACK):
+                if t not in order:
+                    add_tap0(h * HALF, t)
+            add_tap0(h * HALF, order[-1])
+            activate(h * HALF)
+            for s in pieces:
+                if h * HALF < s < (h + 1) * HALF:
+                    for t in range(PACK):
+                        add_tap0(s, t)
+                    activate(s)
+
+        products = [psum.tile([P, n], F32, name=f"product{c}", tag=f"bank0{c}") for c, (s, n) in enumerate(OUT_PIECES)]
+        results = [keep.tile([P, n], F32, name=f"result{s}") for s, n in OUT_PIECES]
+        for c, (s, n) in enumerate(OUT_PIECES):
+            for first in [first for first in pieces if s <= first < s + n]:
+                cols = slice(first - s, first - s + pieces[first])
+                nc.vector.quantize_mx(z_codes[c][:, cols].bitcast(FP8X4), z_plane[c][:, cols], z[first][:].rearrange("p s t -> p (s t)"))
             nc.tensor.matmul_mx(
-                product, w2_codes[:].bitcast(FP4X4), w2_plane[:], z_codes[c][:].bitcast(FP8X4), z_plane[c][:],
+                products[c][:], w2_codes[:].bitcast(FP4X4), w2_plane[:], z_codes[c][:].bitcast(FP8X4), z_plane[c][:],
                 start=True, stop=True,
             )
-
-        add_tap1(0, 0)
-        for t in range(1, PACK):
-            add_tap1(0, t)
-            add_tap0(0, t - 1)
-        add_tap0(0, PACK - 1)
-        activate(0)
-        for t in range(PACK):
-            add_tap1(1, t)
-        for c in (1, 2):
-            for t in range(PACK):
-                add_tap0(c, t)
-            activate(c)
-
-        products = [psum.tile([P, n], F32, name=f"product{c}", tag=f"bank0{c}") for c, (s, n) in enumerate(CHUNKS)]
-        results = [keep.tile([P, n], F32, name=f"result{s}") for s, n in CHUNKS]
-        for c in range(3):
-            multiply(c, products[c][:])
         for c, copy, queue in ((0, nc.scalar.copy, nc.sync), (1, nc.scalar.copy, nc.sync), (2, nc.vector.tensor_copy, nc.scalar)):
-            s, n = CHUNKS[c]
+            s, n = OUT_PIECES[c]
             copy(results[c][:], products[c][:])
             queue.dma_start(out=out[:, s : s + n], in_=results[c][:])

@@ -177,7 +177,7 @@ def tile_picked_dconv_silu_e_kernel(tc, xT, w1, w2_words, w2_scales, taps, offs,
 
         def activate(s):
             nc.scalar.activation(
-                z[s][:].rearrange("p (s i) t -> p s t i", i=4), summed[s][:].rearrange("p t (s i) -> p s t i", i=4), SILU
+                z[s][:].rearrange("p (s i) t -> p s t i", i=2), summed[s][:].rearrange("p t (s i) -> p s t i", i=2), SILU
             )
 
         for h in range(2):

@@ -28,7 +28,7 @@ GPSIMD_SLOTS = (3,)
 SECOND_ORDER = (3, 2, 1, 0)
 W_HALF = H // 2
 M_HALF = W_HALF // PACK
-M_VECTOR = 44
+M_VECTOR = 32
 M_VECTOR_FIRST = 80
 
 
@@ -51,17 +51,16 @@ def tile_picked_dconv_silu_e_kernel(tc, xT, w1, w2_words, w2_scales, taps, offs,
 
         def load_planes(g, j, count):
             rows = xT[g * K_PASS : (g + 1) * K_PASS, :].rearrange("(p j) t -> p j t", j=PACK)
-            loaded = keep.tile([P, count, T], F32, name=f"planes{g}{j}")
+            loaded = keep.tile([P, count, T], F32, name=f"planes{g}{j}", tag=f"planes{g}{j}", align_bytes=64)
             nc.sync.dma_start(out=loaded[:], in_=rows[:, j : j + count, :])
             for i in range(count):
                 planes[g, j + i] = loaded[:, i, :]
 
-        load_planes(0, 0, 1)
+        load_planes(0, 0, 2)
         nc.sync.dma_start(offsets[:], offs)
-        for j in range(1, PACK):
-            load_planes(0, j, 1)
-        for j in range(PACK - 1):
-            load_planes(1, j, 1)
+        load_planes(0, 2, 2)
+        load_planes(1, 0, 2)
+        load_planes(1, 2, 1)
         nc.sync.dma_start(out=w_first[:], in_=w1[0:K_PASS, :].rearrange("(p j) c -> p j c", j=PACK))
         load_planes(1, 3, 1)
         for c in range(2):
@@ -77,27 +76,36 @@ def tile_picked_dconv_silu_e_kernel(tc, xT, w1, w2_words, w2_scales, taps, offs,
         acc = keep.tile([P, PACK, S + 8], F32, name="acc")
         nc.scalar.activation(acc[:, :, 0 : D - 1], zeros[:], SILU)
 
-        picked = [keep.tile([P, S, PACK], BF16, name=f"picked{g}", align_bytes=64) for g in range(2)]
+        gathered = {(g, h): keep.tile([P, PACK, HALF], F32, name=f"gathered{g}{h}") for g in range(2) for h in range(2)}
+        picked = {(g, h): keep.tile([P, HALF, PACK], BF16, name=f"picked{g}{h}", align_bytes=64) for g in range(2) for h in range(2)}
         x_codes = {}
         x_plane = {(g, h): keep.tile([P, HALF], U8, name=f"x_plane{g}{h}", align_bytes=64) for g in range(2) for h in range(2)}
-        dealt = [keep.tile([P, PACK, P, PACK], BF16, name=f"dealt{g}", align_bytes=64) for g in range(2)]
+        dealt = {(g, pair): keep.tile([P, 2, P, PACK], BF16, name=f"dealt{g}{pair}", align_bytes=64) for g in range(2) for pair in range(2)}
         w_codes = [keep.tile([P, H], U32, name=f"w_codes{g}", align_bytes=64) for g in range(2)]
         w_plane = [keep.tile([P, H], U8, name=f"w_plane{g}", align_bytes=64) for g in range(2)]
         hidden = [[psum.tile([P, HALF], F32, name=f"hidden{h}{t}", tag=f"bank{h}{t}") for t in range(PACK)] for h in range(2)]
 
-        def gather(g, j, s, n):
-            nc.vector.tensor_copy(picked[g][:, s : s + n, j], planes[g, j].indirect(offsets[:, s // 16 : (s + n) // 16]))
+        def gather(g, j):
+            for h in range(2):
+                entries = offsets[:, h * HALF // 16 : (h + 1) * HALF // 16]
+                nc.vector.tensor_copy(gathered[g, h][:, j, :], planes[g, j].indirect(entries))
+
+        def weave(g, h, rows):
+            nc.scalar.copy(
+                picked[g, h][:, :, rows].rearrange("p (s i) j -> p s j i", i=2),
+                gathered[g, h][:, rows, :].rearrange("p j (s i) -> p s j i", i=2),
+            )
 
         def quantize_x(g, h, tag):
             x_codes[g, h] = keep.tile([P, HALF], U32, name=f"x_codes{g}{h}", tag=tag, align_bytes=64)
             nc.vector.quantize_mx(
                 x_codes[g, h][:].bitcast(FP8X4), x_plane[g, h][:],
-                picked[g][:, h * HALF : (h + 1) * HALF, :].rearrange("p s j -> p (s j)"),
+                picked[g, h][:].rearrange("p s j -> p (s j)"),
             )
 
-        def deal(copy, g, raw, m_raw, m_count, m_dealt, slots=slice(0, PACK)):
-            src = raw[:].rearrange("p j (m t) -> p m j t", t=PACK)[:, m_raw : m_raw + m_count, :, slots]
-            dst = dealt[g][:].rearrange("p t m j -> p m j t")[:, m_dealt : m_dealt + m_count, :, slots]
+        def deal(copy, g, pair, raw, m_raw, m_count, m_dealt):
+            src = raw[:].rearrange("p j (m t) -> p m j t", t=PACK)[:, m_raw : m_raw + m_count, :, 2 * pair : 2 * pair + 2]
+            dst = dealt[g, pair][:].rearrange("p t m j -> p m j t")[:, m_dealt : m_dealt + m_count, :, :]
             copy(dst, src)
 
         def project(g, h, t):
@@ -108,33 +116,39 @@ def tile_picked_dconv_silu_e_kernel(tc, xT, w1, w2_words, w2_scales, taps, offs,
             )
 
         for j in range(PACK):
-            gather(0, j, 0, S)
+            gather(0, j)
         for h in range(2):
-            quantize_x(0, h, f"x_codes0{h}")
-        for j in range(PACK - 1):
-            gather(1, j, 0, S)
-        for slots in (slice(0, 2), slice(2, 4)):
-            deal(nc.vector.tensor_copy, 0, w_first, 0, M_VECTOR_FIRST, 0, slots)
-            deal(nc.scalar.copy, 0, w_first, M_VECTOR_FIRST, P - M_VECTOR_FIRST, M_VECTOR_FIRST, slots)
+            weave(0, h, slice(0, PACK))
+        quantize_x(0, 0, "x_codes00")
+        for j in range(2):
+            gather(1, j)
+        quantize_x(0, 1, "planes10")
+        for h in range(2):
+            weave(1, h, slice(0, 2))
+        gather(1, 2)
+        for pair in range(2):
+            deal(nc.vector.tensor_copy, 0, pair, w_first, 0, M_VECTOR_FIRST, 0)
+            deal(nc.scalar.copy, 0, pair, w_first, M_VECTOR_FIRST, P - M_VECTOR_FIRST, M_VECTOR_FIRST)
         for pair in range(2):
             cols = slice(pair * 2 * P, (pair + 1) * 2 * P)
             nc.vector.quantize_mx(
-                w_codes[0][:, cols].bitcast(FP8X4), w_plane[0][:, cols],
-                dealt[0][:, 2 * pair : 2 * pair + 2].rearrange("p t m j -> p (t m j)"),
+                w_codes[0][:, cols].bitcast(FP8X4), w_plane[0][:, cols], dealt[0, pair][:].rearrange("p t m j -> p (t m j)")
             )
         for h in range(2):
             for t in range(PACK):
                 project(0, h, t)
+        gather(1, PACK - 1)
         for h in range(2):
-            gather(1, PACK - 1, h * HALF, HALF)
-        quantize_x(1, 0, "x_codes10")
-        deal(nc.scalar.copy, 1, w_last[0], 0, M_HALF, 0)
-        for slots in (slice(0, 2), slice(2, 4)):
-            deal(nc.vector.tensor_copy, 1, w_last[1], 0, M_VECTOR, M_HALF, slots)
-            deal(nc.scalar.copy, 1, w_last[1], M_VECTOR, M_HALF - M_VECTOR, M_HALF + M_VECTOR, slots)
+            weave(1, h, slice(2, PACK))
+        for pair in range(2):
+            deal(nc.vector.tensor_copy, 1, pair, w_last[0], 0, M_HALF, 0)
+        quantize_x(1, 0, "w_last0")
+        deal(nc.vector.tensor_copy, 1, 0, w_last[1], 0, M_HALF, M_HALF)
+        deal(nc.vector.tensor_copy, 1, 1, w_last[1], 0, M_VECTOR, M_HALF)
+        deal(nc.scalar.copy, 1, 1, w_last[1], M_VECTOR, M_HALF - M_VECTOR, M_HALF + M_VECTOR)
         for t in range(PACK):
             cols = slice(t * P, (t + 1) * P)
-            nc.vector.quantize_mx(w_codes[1][:, cols].bitcast(FP8X4), w_plane[1][:, cols], dealt[1][:, t].rearrange("p m j -> p (m j)"))
+            nc.vector.quantize_mx(w_codes[1][:, cols].bitcast(FP8X4), w_plane[1][:, cols], dealt[1, t // 2][:, t % 2].rearrange("p m j -> p (m j)"))
         quantize_x(1, 1, "w_last1")
         for t in range(PACK):
             project(1, 0, t)

@@ -56,11 +56,12 @@ def tile_picked_dconv_silu_e_kernel(tc, xT, w1, w2_words, w2_scales, taps, offs,
             for i in range(count):
                 planes[g, j + i] = loaded[:, i, :]
 
-        load_planes(0, 0, 2)
+        load_planes(0, 0, 1)
         nc.sync.dma_start(offsets[:], offs)
-        load_planes(0, 2, 2)
-        load_planes(1, 0, 2)
-        load_planes(1, 2, 1)
+        for j in range(1, PACK):
+            load_planes(0, j, 1)
+        for j in range(PACK - 1):
+            load_planes(1, j, 1)
         nc.sync.dma_start(out=w_first[:], in_=w1[0:K_PASS, :].rearrange("(p j) c -> p j c", j=PACK))
         load_planes(1, 3, 1)
         for c in range(2):
@@ -122,7 +123,7 @@ def tile_picked_dconv_silu_e_kernel(tc, xT, w1, w2_words, w2_scales, taps, offs,
         quantize_x(0, 0, "x_codes00")
         for j in range(2):
             gather(1, j)
-        quantize_x(0, 1, "planes10")
+        quantize_x(0, 1, "x_codes01")
         for h in range(2):
             weave(1, h, slice(0, 2))
         gather(1, 2)

@@ -28,7 +28,8 @@ GPSIMD_SLOTS = (3,)
 SECOND_ORDER = (3, 2, 1, 0)
 W_HALF = H // 2
 M_HALF = W_HALF // PACK
-M_VECTOR = 32
+WOVEN = (PACK, 2)
+M_VECTOR = 44
 M_VECTOR_FIRST = 80
 
 
@@ -77,7 +78,7 @@ def tile_picked_dconv_silu_e_kernel(tc, xT, w1, w2_words, w2_scales, taps, offs,
         acc = keep.tile([P, PACK, S + 8], F32, name="acc")
         nc.scalar.activation(acc[:, :, 0 : D - 1], zeros[:], SILU)
 
-        gathered = {(g, h): keep.tile([P, PACK, HALF], F32, name=f"gathered{g}{h}") for g in range(2) for h in range(2)}
+        gathered = {(g, h): keep.tile([P, WOVEN[g], HALF], F32, name=f"gathered{g}{h}") for g in range(2) for h in range(2)}
         picked = {(g, h): keep.tile([P, HALF, PACK], BF16, name=f"picked{g}{h}", align_bytes=64) for g in range(2) for h in range(2)}
         x_codes = {}
         x_plane = {(g, h): keep.tile([P, HALF], U8, name=f"x_plane{g}{h}", align_bytes=64) for g in range(2) for h in range(2)}
@@ -89,7 +90,8 @@ def tile_picked_dconv_silu_e_kernel(tc, xT, w1, w2_words, w2_scales, taps, offs,
         def gather(g, j):
             for h in range(2):
                 entries = offsets[:, h * HALF // 16 : (h + 1) * HALF // 16]
-                nc.vector.tensor_copy(gathered[g, h][:, j, :], planes[g, j].indirect(entries))
+                target = gathered[g, h][:, j, :] if j < WOVEN[g] else picked[g, h][:, :, j]
+                nc.vector.tensor_copy(target, planes[g, j].indirect(entries))
 
         def weave(g, h, rows):
             nc.scalar.copy(
@@ -139,14 +141,12 @@ def tile_picked_dconv_silu_e_kernel(tc, xT, w1, w2_words, w2_scales, taps, offs,
             for t in range(PACK):
                 project(0, h, t)
         gather(1, PACK - 1)
-        for h in range(2):
-            weave(1, h, slice(2, PACK))
+        quantize_x(1, 0, "x_codes10")
         for pair in range(2):
-            deal(nc.vector.tensor_copy, 1, pair, w_last[0], 0, M_HALF, 0)
-        quantize_x(1, 0, "w_last0")
-        deal(nc.vector.tensor_copy, 1, 0, w_last[1], 0, M_HALF, M_HALF)
-        deal(nc.vector.tensor_copy, 1, 1, w_last[1], 0, M_VECTOR, M_HALF)
-        deal(nc.scalar.copy, 1, 1, w_last[1], M_VECTOR, M_HALF - M_VECTOR, M_HALF + M_VECTOR)
+            deal(nc.scalar.copy, 1, pair, w_last[0], 0, M_HALF, 0)
+        for pair in range(2):
+            deal(nc.vector.tensor_copy, 1, pair, w_last[1], 0, M_VECTOR, M_HALF)
+            deal(nc.scalar.copy, 1, pair, w_last[1], M_VECTOR, M_HALF - M_VECTOR, M_HALF + M_VECTOR)
         for t in range(PACK):
             cols = slice(t * P, (t + 1) * P)
             nc.vector.quantize_mx(w_codes[1][:, cols].bitcast(FP8X4), w_plane[1][:, cols], dealt[1, t // 2][:, t % 2].rearrange("p m j -> p (m j)"))

@@ -29,7 +29,7 @@ SECOND_ORDER = (3, 2, 1, 0)
 W_HALF = H // 2
 M_HALF = W_HALF // PACK
 WOVEN = (PACK, 2)
-M_VECTOR = 44
+M_VECTOR = (44, 24)
 M_VECTOR_FIRST = 80
 
 
@@ -111,6 +111,11 @@ def tile_picked_dconv_silu_e_kernel(tc, xT, w1, w2_words, w2_scales, taps, offs,
             dst = dealt[g, pair][:].rearrange("p t m j -> p m j t")[:, m_dealt : m_dealt + m_count, :, :]
             copy(dst, src)
 
+        def quantize_w_last(t, m, count):
+            cols = slice(t * P + m, t * P + m + count)
+            values = dealt[1, t // 2][:, t % 2, m : m + count].rearrange("p m j -> p (m j)")
+            nc.vector.quantize_mx(w_codes[1][:, cols].bitcast(FP8X4), w_plane[1][:, cols], values)
+
         def project(g, h, t):
             cols = slice(t * P, (t + 1) * P)
             nc.tensor.matmul_mx(
@@ -144,12 +149,17 @@ def tile_picked_dconv_silu_e_kernel(tc, xT, w1, w2_words, w2_scales, taps, offs,
         quantize_x(1, 0, "x_codes10")
         for pair in range(2):
             deal(nc.scalar.copy, 1, pair, w_last[0], 0, M_HALF, 0)
+        for t in range(2):
+            quantize_w_last(t, 0, M_HALF)
         for pair in range(2):
-            deal(nc.vector.tensor_copy, 1, pair, w_last[1], 0, M_VECTOR, M_HALF)
-            deal(nc.scalar.copy, 1, pair, w_last[1], M_VECTOR, M_HALF - M_VECTOR, M_HALF + M_VECTOR)
-        for t in range(PACK):
-            cols = slice(t * P, (t + 1) * P)
-            nc.vector.quantize_mx(w_codes[1][:, cols].bitcast(FP8X4), w_plane[1][:, cols], dealt[1, t // 2][:, t % 2].rearrange("p m j -> p (m j)"))
+            share = M_VECTOR[pair]
+            deal(nc.vector.tensor_copy, 1, pair, w_last[1], 0, share, M_HALF)
+            deal(nc.scalar.copy, 1, pair, w_last[1], share, M_HALF - share, M_HALF + share)
+        for t in range(2):
+            quantize_w_last(t, M_HALF, M_HALF)
+        nc.vector.quantize_mx(
+            w_codes[1][:, 2 * P :].bitcast(FP8X4), w_plane[1][:, 2 * P :], dealt[1, 1][:].rearrange("p t m j -> p (t m j)")
+        )
         quantize_x(1, 1, "w_last1")
         for t in range(PACK):
             project(1, 0, t)

@@ -184,7 +184,7 @@ def tile_picked_dconv_silu_e_kernel(tc, xT, w1, w2_words, w2_scales, taps, offs,
                 nc.scalar.activation(acc[:, t, HALF + 2 : S + 2], hidden[1][t][:], COPY, scale=tap[:, t, 2:3])
 
         pieces = dict(ACT_PIECES)
-        summed = {s: keep.tile([P, PACK, n], F32, name=f"summed{s}") for s, n in ACT_PIECES}
+        summed = {s: keep.tile([P, n // PACK, PACK, PACK], F32, name=f"summed{s}") for s, n in ACT_PIECES}
         z = {s: keep.tile([P, n, PACK], BF16, name=f"z{s}", align_bytes=64) for s, n in ACT_PIECES}
         z_codes = [keep.tile([P, n], U32, name=f"z_codes{s}", align_bytes=64) for s, n in OUT_PIECES]
         z_plane = [keep.tile([P, n], U8, name=f"z_plane{s}", align_bytes=64) for s, n in OUT_PIECES]
@@ -198,11 +198,14 @@ def tile_picked_dconv_silu_e_kernel(tc, xT, w1, w2_words, w2_scales, taps, offs,
             n = pieces[s]
             bank = hidden[s // HALF][t][:, s % HALF : s % HALF + n]
             before = older[t][:, s - HALF : s - HALF + n] if t in GPSIMD_SLOTS and s >= HALF else acc[:, t, s : s + n]
-            nc.vector.scalar_tensor_tensor(summed[s][:, t, :], bank, tap[:, t, 0:1], before, MULT, ADD)
+            nc.vector.scalar_tensor_tensor(
+                summed[s][:, :, t, :], bank.rearrange("p (s i) -> p s i", i=PACK), tap[:, t, 0:1],
+                before.rearrange("p (s i) -> p s i", i=PACK), MULT, ADD,
+            )
 
         def activate(s):
             nc.scalar.activation(
-                z[s][:].rearrange("p (s i) t -> p s t i", i=2), summed[s][:].rearrange("p t (s i) -> p s t i", i=2), SILU
+                z[s][:].rearrange("p (s i) t -> p s t i", i=PACK), summed[s][:], SILU
             )
 
         for h in range(2):

@@ -28,7 +28,6 @@ GPSIMD_SLOTS = (3,)
 SECOND_ORDER = (3, 2, 1, 0)
 W_HALF = H // 2
 M_HALF = W_HALF // PACK
-WOVEN = (PACK, 2)
 M_VECTOR = (44, 24)
 M_VECTOR_FIRST = 80
 
@@ -50,21 +49,16 @@ def tile_picked_dconv_silu_e_kernel(tc, xT, w1, w2_words, w2_scales, taps, offs,
         nc.gpsimd.memset(w2_plane[:], 0)
         planes = {}
 
-        def load_planes(g, j, count):
+        def load_plane(g, j):
             rows = xT[g * K_PASS : (g + 1) * K_PASS, :].rearrange("(p j) t -> p j t", j=PACK)
-            loaded = keep.tile([P, count, T], F32, name=f"planes{g}{j}", tag=f"planes{g}{j}", align_bytes=64)
-            nc.sync.dma_start(out=loaded[:], in_=rows[:, j : j + count, :])
-            for i in range(count):
-                planes[g, j + i] = loaded[:, i, :]
+            planes[g, j] = keep.tile([P, T], F32, name=f"plane{g}{j}", tag=f"plane{g}{j}", align_bytes=64)
+            nc.sync.dma_start(out=planes[g, j][:], in_=rows[:, j, :])
 
-        load_planes(0, 0, 1)
-        nc.sync.dma_start(offsets[:], offs)
-        for j in range(1, PACK):
-            load_planes(0, j, 1)
-        for j in range(PACK - 1):
-            load_planes(1, j, 1)
         nc.sync.dma_start(out=w_first[:], in_=w1[0:K_PASS, :].rearrange("(p j) c -> p j c", j=PACK))
-        load_planes(1, 3, 1)
+        nc.sync.dma_start(offsets[:], offs)
+        for g in range(2):
+            for j in range(PACK):
+                load_plane(g, j)
         for c in range(2):
             rows = w1[K_PASS:K, :].rearrange("(p j) c -> p j c", j=PACK)
             nc.sync.dma_start(out=w_last[c][:], in_=rows[:, :, c * W_HALF : (c + 1) * W_HALF])
@@ -78,7 +72,7 @@ def tile_picked_dconv_silu_e_kernel(tc, xT, w1, w2_words, w2_scales, taps, offs,
         acc = keep.tile([P, PACK, S + 8], F32, name="acc")
         nc.scalar.activation(acc[:, :, 0 : D - 1], zeros[:], SILU)
 
-        gathered = {(g, h): keep.tile([P, WOVEN[g], HALF], F32, name=f"gathered{g}{h}") for g in range(2) for h in range(2)}
+        gathered = {(g, h): keep.tile([P, PACK, HALF], BF16, name=f"gathered{g}{h}") for g in range(2) for h in range(2)}
         picked = {(g, h): keep.tile([P, HALF, PACK], BF16, name=f"picked{g}{h}", align_bytes=64) for g in range(2) for h in range(2)}
         x_codes = {}
         x_plane = {(g, h): keep.tile([P, HALF], U8, name=f"x_plane{g}{h}", align_bytes=64) for g in range(2) for h in range(2)}
@@ -88,21 +82,21 @@ def tile_picked_dconv_silu_e_kernel(tc, xT, w1, w2_words, w2_scales, taps, offs,
         hidden = [[psum.tile([P, HALF], F32, name=f"hidden{h}{t}", tag=f"bank{h}{t}") for t in range(PACK)] for h in range(2)]
 
         def gather(g, j):
-            for h in range(2):
-                entries = offsets[:, h * HALF // 16 : (h + 1) * HALF // 16]
-                target = gathered[g, h][:, j, :] if j < WOVEN[g] else picked[g, h][:, :, j]
-                nc.vector.tensor_copy(target, planes[g, j].indirect(entries))
+            window = [planes[g, j][:].indirect(offsets[:, h * HALF // 16 : (h + 1) * HALF // 16]) for h in range(2)]
+            in_place = g == 1 and j >= 2
+            nc.vector.tensor_copy(picked[g, 0][:, :, j] if in_place else gathered[g, 0][:, j, :], window[0])
+            nc.scalar.activation(gathered[g, 1][:, j, :], window[1], COPY)
 
         def weave(g, h, rows):
-            nc.scalar.copy(
+            nc.vector.tensor_copy(
                 picked[g, h][:, :, rows].rearrange("p (s i) j -> p s j i", i=2),
                 gathered[g, h][:, rows, :].rearrange("p j (s i) -> p s j i", i=2),
             )
 
-        def quantize_x(g, h, tag):
-            x_codes[g, h] = keep.tile([P, HALF], U32, name=f"x_codes{g}{h}", tag=tag, align_bytes=64)
+        def quantize_x(g, h, codes):
+            x_codes[g, h] = codes
             nc.vector.quantize_mx(
-                x_codes[g, h][:].bitcast(FP8X4), x_plane[g, h][:],
+                codes.bitcast(FP8X4), x_plane[g, h][:],
                 picked[g, h][:].rearrange("p s j -> p (s j)"),
             )
 
@@ -120,20 +114,9 @@ def tile_picked_dconv_silu_e_kernel(tc, xT, w1, w2_words, w2_scales, taps, offs,
             cols = slice(t * P, (t + 1) * P)
             nc.tensor.matmul_mx(
                 hidden[h][t][:], w_codes[g][:, cols].bitcast(FP8X4), w_plane[g][:, cols],
-                x_codes[g, h][:].bitcast(FP8X4), x_plane[g, h][:], start=(g == 0), stop=(g == 1),
+                x_codes[g, h].bitcast(FP8X4), x_plane[g, h][:], start=(g == 0), stop=(g == 1),
             )
 
-        for j in range(PACK):
-            gather(0, j)
-        for h in range(2):
-            weave(0, h, slice(0, PACK))
-        quantize_x(0, 0, "x_codes00")
-        for j in range(2):
-            gather(1, j)
-        quantize_x(0, 1, "x_codes01")
-        for h in range(2):
-            weave(1, h, slice(0, 2))
-        gather(1, 2)
         for pair in range(2):
             deal(nc.vector.tensor_copy, 0, pair, w_first, 0, M_VECTOR_FIRST, 0)
             deal(nc.scalar.copy, 0, pair, w_first, M_VECTOR_FIRST, P - M_VECTOR_FIRST, M_VECTOR_FIRST)
@@ -142,11 +125,24 @@ def tile_picked_dconv_silu_e_kernel(tc, xT, w1, w2_words, w2_scales, taps, offs,
             nc.vector.quantize_mx(
                 w_codes[0][:, cols].bitcast(FP8X4), w_plane[0][:, cols], dealt[0, pair][:].rearrange("p t m j -> p (t m j)")
             )
+        for j in range(PACK):
+            gather(0, j)
+        for h in range(2):
+            weave(0, h, slice(0, PACK))
+        for j in range(2):
+            gather(1, j)
+        for h in range(2):
+            weave(1, h, slice(0, 2))
+        gather(1, 2)
+        first_codes = keep.tile([P, 2, HALF], U32, name="first_codes", tag="plane12", align_bytes=64)
+        for h in range(2):
+            quantize_x(0, h, first_codes[:, h, :])
         for h in range(2):
             for t in range(PACK):
                 project(0, h, t)
         gather(1, PACK - 1)
-        quantize_x(1, 0, "x_codes10")
+        weave(1, 1, slice(2, PACK))
+        quantize_x(1, 0, keep.tile([P, HALF], U32, name="x_codes10", align_bytes=64)[:])
         for pair in range(2):
             deal(nc.scalar.copy, 1, pair, w_last[0], 0, M_HALF, 0)
         for t in range(2):
@@ -160,7 +156,7 @@ def tile_picked_dconv_silu_e_kernel(tc, xT, w1, w2_words, w2_scales, taps, offs,
         nc.vector.quantize_mx(
             w_codes[1][:, 2 * P :].bitcast(FP8X4), w_plane[1][:, 2 * P :], dealt[1, 1][:].rearrange("p t m j -> p (t m j)")
         )
-        quantize_x(1, 1, "w_last1")
+        quantize_x(1, 1, keep.tile([P, HALF], U32, name="x_codes11", tag="w_last1", align_bytes=64)[:])
         for t in range(PACK):
             project(1, 0, t)
         for t in SECOND_ORDER:

@@ -141,10 +141,10 @@ def tile_picked_dconv_silu_e_kernel(tc, xT, w1, w2_words, w2_scales, taps, offs,
             for t in range(PACK):
                 project(0, h, t)
         gather(1, PACK - 1)
-        weave(1, 1, slice(2, PACK))
         quantize_x(1, 0, keep.tile([P, HALF], U32, name="x_codes10", align_bytes=64)[:])
-        for pair in range(2):
-            deal(nc.scalar.copy, 1, pair, w_last[0], 0, M_HALF, 0)
+        weave(1, 1, slice(2, PACK))
+        deal(nc.scalar.copy, 1, 0, w_last[0], 0, M_HALF, 0)
+        deal(nc.vector.tensor_copy, 1, 1, w_last[0], 0, M_HALF, 0)
         for t in range(2):
             quantize_w_last(t, 0, M_HALF)
         for pair in range(2):

@@ -30,6 +30,7 @@ W_HALF = H // 2
 M_HALF = W_HALF // PACK
 M_VECTOR = (44, 24)
 M_VECTOR_FIRST = 80
+M_AHEAD = 36
 
 
 def tile_picked_dconv_silu_e_kernel(tc, xT, w1, w2_words, w2_scales, taps, offs, out):
@@ -40,7 +41,7 @@ def tile_picked_dconv_silu_e_kernel(tc, xT, w1, w2_words, w2_scales, taps, offs,
 
         offsets = keep.tile([P, S // 16], U16, name="offsets")
         w_first = keep.tile([P, PACK, H], F32, name="w_first")
-        w_last = [keep.tile([P, PACK, W_HALF], F32, name=f"w_last{c}", tag=f"w_last{c}", align_bytes=64) for c in range(2)]
+        w_last = keep.tile([P, PACK, H], F32, name="w_last", tag="w_last", align_bytes=64)
         tap = keep.tile([P, PACK, D], F32, name="tap")
         w2_codes = keep.tile([P, 2 * N], U8, name="w2_codes", align_bytes=64)
         w2_plane = keep.tile([P, N], U8, name="w2_plane", align_bytes=64)
@@ -59,9 +60,9 @@ def tile_picked_dconv_silu_e_kernel(tc, xT, w1, w2_words, w2_scales, taps, offs,
         for g in range(2):
             for j in range(PACK):
                 load_plane(g, j)
-        for c in range(2):
-            rows = w1[K_PASS:K, :].rearrange("(p j) c -> p j c", j=PACK)
-            nc.sync.dma_start(out=w_last[c][:], in_=rows[:, :, c * W_HALF : (c + 1) * W_HALF])
+        run = w1[K_PASS:K, :].rearrange("(p j) c -> p (j c)", j=PACK)
+        for cut in (slice(0, PACK * H - W_HALF), slice(PACK * H - W_HALF, PACK * H)):
+            nc.sync.dma_start(out=w_last[:].rearrange("p j c -> p (j c)")[:, cut], in_=run[:, cut])
         nc.sync.dma_start(out=tap[:], in_=taps.rearrange("(p t) d -> p t d", t=PACK))
         nc.sync.dma_start(out=w2_codes[:].bitcast(I32), in_=w2_words[0].bitcast(I32))
         for q in range(4):
@@ -143,20 +144,20 @@ def tile_picked_dconv_silu_e_kernel(tc, xT, w1, w2_words, w2_scales, taps, offs,
         gather(1, PACK - 1)
         quantize_x(1, 0, keep.tile([P, HALF], U32, name="x_codes10", align_bytes=64)[:])
         weave(1, 1, slice(2, PACK))
-        deal(nc.scalar.copy, 1, 0, w_last[0], 0, M_HALF, 0)
-        deal(nc.vector.tensor_copy, 1, 1, w_last[0], 0, M_HALF, 0)
+        deal(nc.vector.tensor_copy, 1, 0, w_last, 0, M_HALF, 0)
+        deal(nc.scalar.copy, 1, 1, w_last, 0, M_AHEAD, 0)
+        cut = M_HALF + M_VECTOR[0]
+        deal(nc.vector.tensor_copy, 1, 0, w_last, M_HALF, M_VECTOR[0], M_HALF)
+        deal(nc.scalar.copy, 1, 0, w_last, cut, P - cut, cut)
+        cut = P - M_VECTOR[1]
+        deal(nc.scalar.copy, 1, 1, w_last, M_AHEAD, cut - M_AHEAD, M_AHEAD)
+        deal(nc.vector.tensor_copy, 1, 1, w_last, cut, M_VECTOR[1], cut)
         for t in range(2):
-            quantize_w_last(t, 0, M_HALF)
-        for pair in range(2):
-            share = M_VECTOR[pair]
-            deal(nc.vector.tensor_copy, 1, pair, w_last[1], 0, share, M_HALF)
-            deal(nc.scalar.copy, 1, pair, w_last[1], share, M_HALF - share, M_HALF + share)
-        for t in range(2):
-            quantize_w_last(t, M_HALF, M_HALF)
+            quantize_w_last(t, 0, P)
         nc.vector.quantize_mx(
             w_codes[1][:, 2 * P :].bitcast(FP8X4), w_plane[1][:, 2 * P :], dealt[1, 1][:].rearrange("p t m j -> p (t m j)")
         )
-        quantize_x(1, 1, keep.tile([P, HALF], U32, name="x_codes11", tag="w_last1", align_bytes=64)[:])
+        quantize_x(1, 1, keep.tile([P, HALF], U32, name="x_codes11", tag="w_last", align_bytes=64)[:])
         for t in range(PACK):
             project(1, 0, t)
         for t in SECOND_ORDER:

@@ -23,7 +23,7 @@ PACK = 4
 K_PASS = P * PACK
 HALF = S // 2
 ACT_PIECES = ((0, 128), (128, 128), (256, 128), (384, 64), (448, 64))
-OUT_PIECES = ((0, 256), (256, 128), (384, 128))
+OUT_PIECES = ((0, 256, 0), (256, 128, 256), (384, 64, 320), (448, 64, 384))
 GPSIMD_SLOTS = (3,)
 SECOND_ORDER = (3, 2, 1, 0)
 W_HALF = H // 2
@@ -183,8 +183,8 @@ def tile_picked_dconv_silu_e_kernel(tc, xT, w1, w2_words, w2_scales, taps, offs,
         pieces = dict(ACT_PIECES)
         summed = {s: keep.tile([P, n // PACK, PACK, PACK], F32, name=f"summed{s}") for s, n in ACT_PIECES}
         z = {s: keep.tile([P, n, PACK], BF16, name=f"z{s}", align_bytes=64) for s, n in ACT_PIECES}
-        z_codes = [keep.tile([P, n], U32, name=f"z_codes{s}", align_bytes=64) for s, n in OUT_PIECES]
-        z_plane = [keep.tile([P, n], U8, name=f"z_plane{s}", align_bytes=64) for s, n in OUT_PIECES]
+        z_codes = keep.tile([P, S], U32, name="z_codes", align_bytes=64)
+        z_plane = keep.tile([P, S], U8, name="z_plane", align_bytes=64)
 
         def add_tap1(h, t):
             n = HALF - 1 if t in GPSIMD_SLOTS else HALF
@@ -222,17 +222,17 @@ def tile_picked_dconv_silu_e_kernel(tc, xT, w1, w2_words, w2_scales, taps, offs,
                         add_tap0(s, t)
                     activate(s)
 
-        products = [psum.tile([P, n], F32, name=f"product{c}", tag=f"bank0{c}") for c, (s, n) in enumerate(OUT_PIECES)]
-        results = [keep.tile([P, n], F32, name=f"result{s}") for s, n in OUT_PIECES]
-        for c, (s, n) in enumerate(OUT_PIECES):
+        products = [psum.tile([P, s + n - start], F32, name=f"product{c}", tag=f"bank0{c}") for c, (s, n, start) in enumerate(OUT_PIECES)]
+        results = [keep.tile([P, n], F32, name=f"result{s}") for s, n, start in OUT_PIECES]
+        for c, (s, n, start) in enumerate(OUT_PIECES):
             for first in [first for first in pieces if s <= first < s + n]:
-                cols = slice(first - s, first - s + pieces[first])
-                nc.vector.quantize_mx(z_codes[c][:, cols].bitcast(FP8X4), z_plane[c][:, cols], z[first][:].rearrange("p s t -> p (s t)"))
+                cols = slice(first, first + pieces[first])
+                nc.vector.quantize_mx(z_codes[:, cols].bitcast(FP8X4), z_plane[:, cols], z[first][:].rearrange("p s t -> p (s t)"))
             nc.tensor.matmul_mx(
-                products[c][:], w2_codes[:].bitcast(FP4X4), w2_plane[:], z_codes[c][:].bitcast(FP8X4), z_plane[c][:],
-                start=True, stop=True,
+                products[c][:], w2_codes[:].bitcast(FP4X4), w2_plane[:],
+                z_codes[:, start : s + n].bitcast(FP8X4), z_plane[:, start : s + n], start=True, stop=True,
             )
-        for c, copy, queue in ((0, nc.scalar.copy, nc.sync), (1, nc.scalar.copy, nc.sync), (2, nc.vector.tensor_copy, nc.scalar)):
-            s, n = OUT_PIECES[c]
-            copy(results[c][:], products[c][:])
+        for c, (s, n, start) in enumerate(OUT_PIECES):
+            copy, queue = (nc.vector.tensor_copy, nc.scalar) if c == len(OUT_PIECES) - 1 else (nc.scalar.copy, nc.sync)
+            copy(results[c][:], products[c][:, s - start :])
             queue.dma_start(out=out[:, s : s + n], in_=results[c][:])

@@ -24,8 +24,11 @@ K_PASS = P * PACK
 HALF = S // 2
 ACT_PIECES = ((0, 128), (128, 128), (256, 128), (384, 64), (448, 64))
 OUT_PIECES = ((0, 256, 0), (256, 128, 256), (384, 64, 320), (448, 64, 384))
-GPSIMD_SLOTS = (3,)
-SECOND_ORDER = (3, 2, 1, 0)
+GPSIMD_SLOTS = (0,)
+SECOND_ORDER = (0, 1, 2, 3)
+BANK_ORDER = ((0, 0), (0, 1), (1, 0), (0, 2), (0, 3), (1, 1), (1, 2), (1, 3))
+VECTOR_BANK = (0, 1)
+ADDED_SLOT = 1
 W_HALF = H // 2
 M_HALF = W_HALF // PACK
 M_VECTOR = (44, 24)
@@ -48,6 +51,8 @@ def tile_picked_dconv_silu_e_kernel(tc, xT, w1, w2_words, w2_scales, taps, offs,
         zeros = keep.tile([P, PACK, D - 1], F32, name="zeros")
         nc.gpsimd.memset(zeros[:], 0.0)
         nc.gpsimd.memset(w2_plane[:], 0)
+        middle = keep.tile([P, HALF], F32, name="middle")
+        nc.gpsimd.memset(middle[:, 0:1], 0.0)
         planes = {}
 
         def load_plane(g, j):
@@ -73,8 +78,8 @@ def tile_picked_dconv_silu_e_kernel(tc, xT, w1, w2_words, w2_scales, taps, offs,
         acc = keep.tile([P, PACK, S + 8], F32, name="acc")
         nc.scalar.activation(acc[:, :, 0 : D - 1], zeros[:], SILU)
 
-        gathered = {(g, h): keep.tile([P, PACK, HALF], BF16, name=f"gathered{g}{h}") for g in range(2) for h in range(2)}
-        picked = {(g, h): keep.tile([P, HALF, PACK], BF16, name=f"picked{g}{h}", align_bytes=64) for g in range(2) for h in range(2)}
+        gathered = {(g, h): keep.tile([P, PACK, HALF], BF16, name=f"gathered{g}{h}", tag=f"gathered{g}{h}", align_bytes=64) for g in range(2) for h in range(2)}
+        picked = {(g, h): keep.tile([P, HALF, PACK], BF16, name=f"picked{g}{h}", align_bytes=64) for g in range(2) for h in range(2) if g or h}
         x_codes = {}
         x_plane = {(g, h): keep.tile([P, HALF], U8, name=f"x_plane{g}{h}", align_bytes=64) for g in range(2) for h in range(2)}
         dealt = {(g, pair): keep.tile([P, 2, P, PACK], BF16, name=f"dealt{g}{pair}", align_bytes=64) for g in range(2) for pair in range(2)}
@@ -128,22 +133,23 @@ def tile_picked_dconv_silu_e_kernel(tc, xT, w1, w2_words, w2_scales, taps, offs,
             )
         for j in range(PACK):
             gather(0, j)
-        for h in range(2):
-            weave(0, h, slice(0, PACK))
+        weave(0, 1, slice(0, PACK))
         for j in range(2):
             gather(1, j)
         for h in range(2):
             weave(1, h, slice(0, 2))
         gather(1, 2)
-        first_codes = keep.tile([P, 2, HALF], U32, name="first_codes", tag="plane12", align_bytes=64)
-        for h in range(2):
-            quantize_x(0, h, first_codes[:, h, :])
-        for h in range(2):
+        picked[0, 0] = keep.tile([P, HALF, PACK], BF16, name="picked00", tag="plane12", align_bytes=64)
+        weave(0, 0, slice(0, PACK))
+        quantize_x(0, 1, keep.tile([P, HALF], U32, name="x_codes01", tag="gathered00", align_bytes=64)[:])
+        quantize_x(0, 0, keep.tile([P, HALF], U32, name="x_codes00", align_bytes=64)[:])
+        for h in (1, 0):
             for t in range(PACK):
                 project(0, h, t)
         gather(1, PACK - 1)
-        quantize_x(1, 0, keep.tile([P, HALF], U32, name="x_codes10", align_bytes=64)[:])
         weave(1, 1, slice(2, PACK))
+        quantize_x(1, 0, keep.tile([P, HALF], U32, name="x_codes10", tag="plane13", align_bytes=64)[:])
+        quantize_x(1, 1, keep.tile([P, HALF], U32, name="x_codes11", align_bytes=64)[:])
         deal(nc.vector.tensor_copy, 1, 0, w_last, 0, M_HALF, 0)
         deal(nc.scalar.copy, 1, 1, w_last, 0, M_AHEAD, 0)
         cut = M_HALF + M_VECTOR[0]
@@ -157,28 +163,28 @@ def tile_picked_dconv_silu_e_kernel(tc, xT, w1, w2_words, w2_scales, taps, offs,
         nc.vector.quantize_mx(
             w_codes[1][:, 2 * P :].bitcast(FP8X4), w_plane[1][:, 2 * P :], dealt[1, 1][:].rearrange("p t m j -> p (t m j)")
         )
-        quantize_x(1, 1, keep.tile([P, HALF], U32, name="x_codes11", tag="w_last", align_bytes=64)[:])
-        for t in range(PACK):
-            project(1, 0, t)
-        for t in SECOND_ORDER:
-            project(1, 1, t)
+        for h, t in BANK_ORDER:
+            project(1, h, t)
 
         plain = {t: keep.tile([P, HALF + 8], F32, name=f"plain{t}") for t in GPSIMD_SLOTS}
-        older = {t: keep.tile([P, HALF], F32, name=f"older{t}") for t in GPSIMD_SLOTS}
-        for t in range(PACK):
-            n = HALF - 2 if t in GPSIMD_SLOTS else HALF
-            nc.scalar.activation(acc[:, t, 2 : n + 2], hidden[0][t][:, :n], COPY, scale=tap[:, t, 2:3])
-            if t in GPSIMD_SLOTS:
-                nc.scalar.copy(plain[t][:, 0:2], hidden[0][t][:, n:])
-        for t in SECOND_ORDER:
-            if t in GPSIMD_SLOTS:
+        older = {t: keep.tile([P, HALF], F32, name=f"older{t}") for t in (*GPSIMD_SLOTS, ADDED_SLOT)}
+        for h, t in BANK_ORDER:
+            n = HALF - 2 if h == 1 or t in GPSIMD_SLOTS else HALF
+            first = h * HALF + 2
+            if h == 1 and t in GPSIMD_SLOTS:
                 scaled = keep.tile([P, HALF], F32, name=f"scaled{t}")
                 nc.scalar.copy(plain[t][:, 2 : HALF + 1], hidden[1][t][:, : HALF - 1])
                 nc.gpsimd.tensor_scalar(older[t][:], plain[t][:, 0:HALF], tap[:, t, 2:3], 0.0, MULT, ADD)
                 nc.gpsimd.tensor_scalar(scaled[:], plain[t][:, 1 : HALF + 1], tap[:, t, 1:2], 0.0, MULT, ADD)
                 nc.gpsimd.tensor_tensor(older[t][:], older[t][:], scaled[:], ADD)
+            elif (h, t) == VECTOR_BANK:
+                nc.vector.tensor_scalar(acc[:, t, first : first + n], hidden[h][t][:, :n], tap[:, t, 2:3], None, MULT)
             else:
-                nc.scalar.activation(acc[:, t, HALF + 2 : S + 2], hidden[1][t][:], COPY, scale=tap[:, t, 2:3])
+                nc.scalar.activation(acc[:, t, first : first + n], hidden[h][t][:, :n], COPY, scale=tap[:, t, 2:3])
+                if t in GPSIMD_SLOTS:
+                    nc.scalar.copy(plain[t][:, 0:2], hidden[0][t][:, n:])
+                if (h, t) == (1, ADDED_SLOT):
+                    nc.scalar.activation(middle[:, 1:], hidden[h][t][:, : HALF - 1], COPY, scale=tap[:, t, 1:2])
 
         pieces = dict(ACT_PIECES)
         summed = {s: keep.tile([P, n // PACK, PACK, PACK], F32, name=f"summed{s}") for s, n in ACT_PIECES}
@@ -187,14 +193,14 @@ def tile_picked_dconv_silu_e_kernel(tc, xT, w1, w2_words, w2_scales, taps, offs,
         z_plane = keep.tile([P, S], U8, name="z_plane", align_bytes=64)
 
         def add_tap1(h, t):
-            n = HALF - 1 if t in GPSIMD_SLOTS else HALF
+            n = HALF - 1 if h == 1 or t in GPSIMD_SLOTS else HALF
             window = acc[:, t, h * HALF + 1 : h * HALF + n + 1]
             nc.vector.scalar_tensor_tensor(window, hidden[h][t][:, :n], tap[:, t, 1:2], window, MULT, ADD)
 
         def add_tap0(s, t):
             n = pieces[s]
             bank = hidden[s // HALF][t][:, s % HALF : s % HALF + n]
-            before = older[t][:, s - HALF : s - HALF + n] if t in GPSIMD_SLOTS and s >= HALF else acc[:, t, s : s + n]
+            before = older[t][:, s - HALF : s - HALF + n] if t in older and s >= HALF else acc[:, t, s : s + n]
             nc.vector.scalar_tensor_tensor(
                 summed[s][:, :, t, :], bank.rearrange("p (s i) -> p s i", i=PACK), tap[:, t, 0:1],
                 before.rearrange("p (s i) -> p s i", i=PACK), MULT, ADD,
@@ -205,22 +211,26 @@ def tile_picked_dconv_silu_e_kernel(tc, xT, w1, w2_words, w2_scales, taps, offs,
                 z[s][:].rearrange("p (s i) t -> p s t i", i=PACK), summed[s][:], SILU
             )
 
-        for h in range(2):
-            order = [t for t in (range(PACK), SECOND_ORDER)[h] if h == 0 or t not in GPSIMD_SLOTS]
-            add_tap1(h, order[0])
-            for before, t in zip(order, order[1:]):
-                add_tap1(h, t)
-                add_tap0(h * HALF, before)
-            for t in range(PACK):
-                if t not in order:
-                    add_tap0(h * HALF, t)
-            add_tap0(h * HALF, order[-1])
-            activate(h * HALF)
-            for s in pieces:
-                if h * HALF < s < (h + 1) * HALF:
-                    for t in range(PACK):
-                        add_tap0(s, t)
-                    activate(s)
+        def finish(s, order):
+            for t in order:
+                add_tap0(s, t)
+            activate(s)
+
+        add_tap1(0, 0)
+        for t in range(1, PACK):
+            add_tap1(0, t)
+            add_tap0(0, t - 1)
+        add_tap0(0, PACK - 1)
+        activate(0)
+        for cols in (slice(0, P), slice(P, HALF)):
+            own = acc[:, ADDED_SLOT, HALF + cols.start : HALF + cols.stop]
+            nc.gpsimd.tensor_tensor(older[ADDED_SLOT][:, cols], own, middle[:, cols], ADD)
+        finish(P, range(PACK))
+        for t in range(PACK):
+            if t not in older:
+                add_tap1(1, t)
+        for s in (HALF, 384, 448):
+            finish(s, (0, 2, 3, 1))
 
         products = [psum.tile([P, s + n - start], F32, name=f"product{c}", tag=f"bank0{c}") for c, (s, n, start) in enumerate(OUT_PIECES)]
         results = [keep.tile([P, n], F32, name=f"result{s}") for s, n, start in OUT_PIECES]

@@ -31,7 +31,7 @@ VECTOR_BANK = (0, 1)
 ADDED_SLOT = 1
 W_HALF = H // 2
 M_HALF = W_HALF // PACK
-M_VECTOR = (44, 24)
+M_VECTOR = (40, 56)
 M_VECTOR_FIRST = 80
 M_AHEAD = 36
 
@@ -79,7 +79,7 @@ def tile_picked_dconv_silu_e_kernel(tc, xT, w1, w2_words, w2_scales, taps, offs,
         nc.scalar.activation(acc[:, :, 0 : D - 1], zeros[:], SILU)
 
         gathered = {(g, h): keep.tile([P, PACK, HALF], BF16, name=f"gathered{g}{h}", tag=f"gathered{g}{h}", align_bytes=64) for g in range(2) for h in range(2)}
-        picked = {(g, h): keep.tile([P, HALF, PACK], BF16, name=f"picked{g}{h}", align_bytes=64) for g in range(2) for h in range(2) if g or h}
+        picked = {(g, h): keep.tile([P, HALF, PACK], BF16, name=f"picked{g}{h}", align_bytes=64) for g in range(2) for h in range(2)}
         x_codes = {}
         x_plane = {(g, h): keep.tile([P, HALF], U8, name=f"x_plane{g}{h}", align_bytes=64) for g in range(2) for h in range(2)}
         dealt = {(g, pair): keep.tile([P, 2, P, PACK], BF16, name=f"dealt{g}{pair}", align_bytes=64) for g in range(2) for pair in range(2)}
@@ -133,30 +133,30 @@ def tile_picked_dconv_silu_e_kernel(tc, xT, w1, w2_words, w2_scales, taps, offs,
             )
         for j in range(PACK):
             gather(0, j)
-        weave(0, 1, slice(0, PACK))
+        for h in range(2):
+            weave(0, h, slice(0, PACK))
         for j in range(2):
             gather(1, j)
         for h in range(2):
             weave(1, h, slice(0, 2))
         gather(1, 2)
-        picked[0, 0] = keep.tile([P, HALF, PACK], BF16, name="picked00", tag="plane12", align_bytes=64)
-        weave(0, 0, slice(0, PACK))
-        quantize_x(0, 1, keep.tile([P, HALF], U32, name="x_codes01", tag="gathered00", align_bytes=64)[:])
-        quantize_x(0, 0, keep.tile([P, HALF], U32, name="x_codes00", align_bytes=64)[:])
-        for h in (1, 0):
+        first_codes = keep.tile([P, 2, HALF], U32, name="first_codes", tag="plane12", align_bytes=64)
+        for h in range(2):
+            quantize_x(0, h, first_codes[:, h, :])
+        for h in range(2):
             for t in range(PACK):
                 project(0, h, t)
         gather(1, PACK - 1)
         weave(1, 1, slice(2, PACK))
         quantize_x(1, 0, keep.tile([P, HALF], U32, name="x_codes10", tag="plane13", align_bytes=64)[:])
         quantize_x(1, 1, keep.tile([P, HALF], U32, name="x_codes11", align_bytes=64)[:])
-        deal(nc.vector.tensor_copy, 1, 0, w_last, 0, M_HALF, 0)
-        deal(nc.scalar.copy, 1, 1, w_last, 0, M_AHEAD, 0)
+        deal(nc.vector.tensor_copy, 1, 0, w_last, 0, M_AHEAD, 0)
+        deal(nc.scalar.copy, 1, 0, w_last, M_AHEAD, M_HALF - M_AHEAD, M_AHEAD)
         cut = M_HALF + M_VECTOR[0]
         deal(nc.vector.tensor_copy, 1, 0, w_last, M_HALF, M_VECTOR[0], M_HALF)
         deal(nc.scalar.copy, 1, 0, w_last, cut, P - cut, cut)
         cut = P - M_VECTOR[1]
-        deal(nc.scalar.copy, 1, 1, w_last, M_AHEAD, cut - M_AHEAD, M_AHEAD)
+        deal(nc.scalar.copy, 1, 1, w_last, 0, cut, 0)
         deal(nc.vector.tensor_copy, 1, 1, w_last, cut, M_VECTOR[1], cut)
         for t in range(2):
             quantize_w_last(t, 0, P)

@@ -23,7 +23,7 @@ PACK = 4
 K_PASS = P * PACK
 HALF = S // 2
 ACT_PIECES = ((0, 128), (128, 128), (256, 128), (384, 64), (448, 64))
-OUT_PIECES = ((0, 256, 0), (256, 128, 256), (384, 64, 320), (448, 64, 384))
+OUT_PIECES = ((0, 256), (256, 128), (384, 128))
 GPSIMD_SLOTS = (0,)
 SECOND_ORDER = (0, 1, 2, 3)
 BANK_ORDER = ((0, 0), (0, 1), (1, 0), (0, 2), (0, 3), (1, 1), (1, 2), (1, 3))
@@ -189,8 +189,8 @@ def tile_picked_dconv_silu_e_kernel(tc, xT, w1, w2_words, w2_scales, taps, offs,
         pieces = dict(ACT_PIECES)
         summed = {s: keep.tile([P, n // PACK, PACK, PACK], F32, name=f"summed{s}") for s, n in ACT_PIECES}
         z = {s: keep.tile([P, n, PACK], BF16, name=f"z{s}", align_bytes=64) for s, n in ACT_PIECES}
-        z_codes = keep.tile([P, S], U32, name="z_codes", align_bytes=64)
-        z_plane = keep.tile([P, S], U8, name="z_plane", align_bytes=64)
+        z_codes = [keep.tile([P, n], U32, name=f"z_codes{s}", align_bytes=64) for s, n in OUT_PIECES]
+        z_plane = [keep.tile([P, n], U8, name=f"z_plane{s}", align_bytes=64) for s, n in OUT_PIECES]
 
         def add_tap1(h, t):
             n = HALF - 1 if h == 1 or t in GPSIMD_SLOTS else HALF
@@ -232,17 +232,17 @@ def tile_picked_dconv_silu_e_kernel(tc, xT, w1, w2_words, w2_scales, taps, offs,
         for s in (HALF, 384, 448):
             finish(s, (0, 2, 3, 1))
 
-        products = [psum.tile([P, s + n - start], F32, name=f"product{c}", tag=f"bank0{c}") for c, (s, n, start) in enumerate(OUT_PIECES)]
-        results = [keep.tile([P, n], F32, name=f"result{s}") for s, n, start in OUT_PIECES]
-        for c, (s, n, start) in enumerate(OUT_PIECES):
+        products = [psum.tile([P, n], F32, name=f"product{c}", tag=f"bank0{c}") for c, (s, n) in enumerate(OUT_PIECES)]
+        results = [keep.tile([P, n], F32, name=f"result{s}") for s, n in OUT_PIECES]
+        for c, (s, n) in enumerate(OUT_PIECES):
             for first in [first for first in pieces if s <= first < s + n]:
-                cols = slice(first, first + pieces[first])
-                nc.vector.quantize_mx(z_codes[:, cols].bitcast(FP8X4), z_plane[:, cols], z[first][:].rearrange("p s t -> p (s t)"))
+                cols = slice(first - s, first - s + pieces[first])
+                nc.vector.quantize_mx(z_codes[c][:, cols].bitcast(FP8X4), z_plane[c][:, cols], z[first][:].rearrange("p s t -> p (s t)"))
             nc.tensor.matmul_mx(
-                products[c][:], w2_codes[:].bitcast(FP4X4), w2_plane[:],
-                z_codes[:, start : s + n].bitcast(FP8X4), z_plane[:, start : s + n], start=True, stop=True,
+                products[c][:], w2_codes[:].bitcast(FP4X4), w2_plane[:], z_codes[c][:].bitcast(FP8X4), z_plane[c][:],
+                start=True, stop=True,
             )
-        for c, (s, n, start) in enumerate(OUT_PIECES):
-            copy, queue = (nc.vector.tensor_copy, nc.scalar) if c == len(OUT_PIECES) - 1 else (nc.scalar.copy, nc.sync)
-            copy(results[c][:], products[c][:, s - start :])
+        for c, copy, queue in ((0, nc.scalar.copy, nc.sync), (1, nc.scalar.copy, nc.sync), (2, nc.vector.tensor_copy, nc.scalar)):
+            s, n = OUT_PIECES[c]
+            copy(results[c][:], products[c][:])
             queue.dma_start(out=out[:, s : s + n], in_=results[c][:])

@@ -23,12 +23,14 @@ PACK = 4
 K_PASS = P * PACK
 HALF = S // 2
 ACT_PIECES = ((0, 128), (128, 128), (256, 128), (384, 64), (448, 64))
-OUT_PIECES = ((0, 256), (256, 128), (384, 128))
+OUT_PIECES = ((0, 128), (128, 128), (256, 128), (384, 128))
+STORES = ((0, 256), (256, 128), (384, 128))
 GPSIMD_SLOTS = (0,)
 SECOND_ORDER = (0, 1, 2, 3)
 BANK_ORDER = ((0, 0), (0, 1), (1, 0), (0, 2), (0, 3), (1, 1), (1, 2), (1, 3))
 VECTOR_BANK = (0, 1)
 ADDED_SLOT = 1
+LATE_SLOT = 2
 W_HALF = H // 2
 M_HALF = W_HALF // PACK
 M_VECTOR = (40, 56)
@@ -51,8 +53,8 @@ def tile_picked_dconv_silu_e_kernel(tc, xT, w1, w2_words, w2_scales, taps, offs,
         zeros = keep.tile([P, PACK, D - 1], F32, name="zeros")
         nc.gpsimd.memset(zeros[:], 0.0)
         nc.gpsimd.memset(w2_plane[:], 0)
-        middle = keep.tile([P, HALF], F32, name="middle")
-        nc.gpsimd.memset(middle[:, 0:1], 0.0)
+        middle = keep.tile([P, 2, HALF], F32, name="middle")
+        nc.gpsimd.memset(middle[:, 0, 0:1], 0.0)
         planes = {}
 
         def load_plane(g, j):
@@ -167,16 +169,18 @@ def tile_picked_dconv_silu_e_kernel(tc, xT, w1, w2_words, w2_scales, taps, offs,
             project(1, h, t)
 
         plain = {t: keep.tile([P, HALF + 8], F32, name=f"plain{t}") for t in GPSIMD_SLOTS}
-        older = {t: keep.tile([P, HALF], F32, name=f"older{t}") for t in (*GPSIMD_SLOTS, ADDED_SLOT)}
+        older = {t: keep.tile([P, HALF], F32, name=f"older{t}")[:] for t in GPSIMD_SLOTS}
+        added = keep.tile([P, 2, HALF], F32, name="added")
+        older[ADDED_SLOT], older[LATE_SLOT] = added[:, 0, :], added[:, 1, :]
         for h, t in BANK_ORDER:
             n = HALF - 2 if h == 1 or t in GPSIMD_SLOTS else HALF
             first = h * HALF + 2
             if h == 1 and t in GPSIMD_SLOTS:
                 scaled = keep.tile([P, HALF], F32, name=f"scaled{t}")
                 nc.scalar.copy(plain[t][:, 2 : HALF + 1], hidden[1][t][:, : HALF - 1])
-                nc.gpsimd.tensor_scalar(older[t][:], plain[t][:, 0:HALF], tap[:, t, 2:3], 0.0, MULT, ADD)
+                nc.gpsimd.tensor_scalar(older[t], plain[t][:, 0:HALF], tap[:, t, 2:3], 0.0, MULT, ADD)
                 nc.gpsimd.tensor_scalar(scaled[:], plain[t][:, 1 : HALF + 1], tap[:, t, 1:2], 0.0, MULT, ADD)
-                nc.gpsimd.tensor_tensor(older[t][:], older[t][:], scaled[:], ADD)
+                nc.gpsimd.tensor_tensor(older[t], older[t], scaled[:], ADD)
             elif (h, t) == VECTOR_BANK:
                 nc.vector.tensor_scalar(acc[:, t, first : first + n], hidden[h][t][:, :n], tap[:, t, 2:3], None, MULT)
             else:
@@ -184,7 +188,9 @@ def tile_picked_dconv_silu_e_kernel(tc, xT, w1, w2_words, w2_scales, taps, offs,
                 if t in GPSIMD_SLOTS:
                     nc.scalar.copy(plain[t][:, 0:2], hidden[0][t][:, n:])
                 if (h, t) == (1, ADDED_SLOT):
-                    nc.scalar.activation(middle[:, 1:], hidden[h][t][:, : HALF - 1], COPY, scale=tap[:, t, 1:2])
+                    nc.scalar.activation(middle[:, 0, 1:], hidden[h][t][:, : HALF - 1], COPY, scale=tap[:, t, 1:2])
+                if (h, t) == (1, LATE_SLOT):
+                    nc.scalar.activation(middle[:, 1, P:], hidden[h][t][:, P - 1 : HALF - 1], COPY, scale=tap[:, t, 1:2])
 
         pieces = dict(ACT_PIECES)
         summed = {s: keep.tile([P, n // PACK, PACK, PACK], F32, name=f"summed{s}") for s, n in ACT_PIECES}
@@ -200,7 +206,7 @@ def tile_picked_dconv_silu_e_kernel(tc, xT, w1, w2_words, w2_scales, taps, offs,
         def add_tap0(s, t):
             n = pieces[s]
             bank = hidden[s // HALF][t][:, s % HALF : s % HALF + n]
-            before = older[t][:, s - HALF : s - HALF + n] if t in older and s >= HALF else acc[:, t, s : s + n]
+            before = older[t][:, s - HALF : s - HALF + n] if t in older and s >= (HALF + P if t == LATE_SLOT else HALF) else acc[:, t, s : s + n]
             nc.vector.scalar_tensor_tensor(
                 summed[s][:, :, t, :], bank.rearrange("p (s i) -> p s i", i=PACK), tap[:, t, 0:1],
                 before.rearrange("p (s i) -> p s i", i=PACK), MULT, ADD,
@@ -222,18 +228,20 @@ def tile_picked_dconv_silu_e_kernel(tc, xT, w1, w2_words, w2_scales, taps, offs,
             add_tap0(0, t - 1)
         add_tap0(0, PACK - 1)
         activate(0)
-        for cols in (slice(0, P), slice(P, HALF)):
-            own = acc[:, ADDED_SLOT, HALF + cols.start : HALF + cols.stop]
-            nc.gpsimd.tensor_tensor(older[ADDED_SLOT][:, cols], own, middle[:, cols], ADD)
+        for slots, cols in ((1, slice(0, P)), (2, slice(P, 192)), (2, slice(192, HALF))):
+            own = acc[:, ADDED_SLOT : ADDED_SLOT + slots, HALF + cols.start : HALF + cols.stop]
+            nc.gpsimd.tensor_tensor(added[:, :slots, cols], own, middle[:, :slots, cols], ADD)
         finish(P, range(PACK))
+        window = acc[:, LATE_SLOT, HALF + 1 : HALF + P]
+        nc.vector.scalar_tensor_tensor(window, hidden[1][LATE_SLOT][:, : P - 1], tap[:, LATE_SLOT, 1:2], window, MULT, ADD)
         for t in range(PACK):
             if t not in older:
                 add_tap1(1, t)
         for s in (HALF, 384, 448):
-            finish(s, (0, 2, 3, 1))
+            finish(s, (0, 2, 1, 3) if s == HALF else (0, 3, 1, 2))
 
         products = [psum.tile([P, n], F32, name=f"product{c}", tag=f"bank0{c}") for c, (s, n) in enumerate(OUT_PIECES)]
-        results = [keep.tile([P, n], F32, name=f"result{s}") for s, n in OUT_PIECES]
+        results = {s: keep.tile([P, n], F32, name=f"result{s}") for s, n in STORES}
         for c, (s, n) in enumerate(OUT_PIECES):
             for first in [first for first in pieces if s <= first < s + n]:
                 cols = slice(first - s, first - s + pieces[first])
@@ -242,7 +250,9 @@ def tile_picked_dconv_silu_e_kernel(tc, xT, w1, w2_words, w2_scales, taps, offs,
                 products[c][:], w2_codes[:].bitcast(FP4X4), w2_plane[:], z_codes[c][:].bitcast(FP8X4), z_plane[c][:],
                 start=True, stop=True,
             )
-        for c, copy, queue in ((0, nc.scalar.copy, nc.sync), (1, nc.scalar.copy, nc.sync), (2, nc.vector.tensor_copy, nc.scalar)):
-            s, n = OUT_PIECES[c]
-            copy(results[c][:], products[c][:])
-            queue.dma_start(out=out[:, s : s + n], in_=results[c][:])
+        for first, width in STORES:
+            copy, queue = (nc.vector.tensor_copy, nc.scalar) if first + width == S else (nc.scalar.copy, nc.sync)
+            for c, (s, n) in enumerate(OUT_PIECES):
+                if first <= s < first + width:
+                    copy(results[first][:, s - first : s - first + n], products[c][:])
+            queue.dma_start(out=out[:, first : first + width], in_=results[first][:])

@@ -251,8 +251,7 @@ def tile_picked_dconv_silu_e_kernel(tc, xT, w1, w2_words, w2_scales, taps, offs,
                 start=True, stop=True,
             )
         for first, width in STORES:
-            copy, queue = (nc.vector.tensor_copy, nc.scalar) if first + width == S else (nc.scalar.copy, nc.sync)
             for c, (s, n) in enumerate(OUT_PIECES):
                 if first <= s < first + width:
-                    copy(results[first][:, s - first : s - first + n], products[c][:])
-            queue.dma_start(out=out[:, first : first + width], in_=results[first][:])
+                    nc.scalar.copy(results[first][:, s - first : s - first + n], products[c][:])
+            nc.sync.dma_start(out=out[:, first : first + width], in_=results[first][:])

@@ -64,9 +64,10 @@ def tile_picked_dconv_silu_e_kernel(tc, xT, w1, w2_words, w2_scales, taps, offs,
 
         nc.sync.dma_start(out=w_first[:], in_=w1[0:K_PASS, :].rearrange("(p j) c -> p j c", j=PACK))
         nc.sync.dma_start(offsets[:], offs)
-        for g in range(2):
-            for j in range(PACK):
-                load_plane(g, j)
+        first_x = keep.tile([P, PACK, T], F32, name="first_x", align_bytes=64)
+        nc.sync.dma_start(out=first_x[:], in_=xT[0:K_PASS, :].rearrange("(p j) t -> p j t", j=PACK))
+        for j in range(PACK):
+            load_plane(1, j)
         run = w1[K_PASS:K, :].rearrange("(p j) c -> p (j c)", j=PACK)
         for cut in (slice(0, PACK * H - W_HALF), slice(PACK * H - W_HALF, PACK * H)):
             nc.sync.dma_start(out=w_last[:].rearrange("p j c -> p (j c)")[:, cut], in_=run[:, cut])
@@ -80,7 +81,7 @@ def tile_picked_dconv_silu_e_kernel(tc, xT, w1, w2_words, w2_scales, taps, offs,
         acc = keep.tile([P, PACK, S + 8], F32, name="acc")
         nc.scalar.activation(acc[:, :, 0 : D - 1], zeros[:], SILU)
 
-        gathered = {(g, h): keep.tile([P, PACK, HALF], BF16, name=f"gathered{g}{h}", tag=f"gathered{g}{h}", align_bytes=64) for g in range(2) for h in range(2)}
+        gathered = {(g, h): keep.tile([P, PACK, HALF], BF16 if g else F32, name=f"gathered{g}{h}", tag=f"gathered{g}{h}", align_bytes=64) for g in range(2) for h in range(2)}
         picked = {(g, h): keep.tile([P, HALF, PACK], BF16, name=f"picked{g}{h}", align_bytes=64) for g in range(2) for h in range(2)}
         x_codes = {}
         x_plane = {(g, h): keep.tile([P, HALF], U8, name=f"x_plane{g}{h}", align_bytes=64) for g in range(2) for h in range(2)}
@@ -90,7 +91,8 @@ def tile_picked_dconv_silu_e_kernel(tc, xT, w1, w2_words, w2_scales, taps, offs,
         hidden = [[psum.tile([P, HALF], F32, name=f"hidden{h}{t}", tag=f"bank{h}{t}") for t in range(PACK)] for h in range(2)]
 
         def gather(g, j):
-            window = [planes[g, j][:].indirect(offsets[:, h * HALF // 16 : (h + 1) * HALF // 16]) for h in range(2)]
+            plane = planes[g, j][:] if g else first_x[:, j, :]
+            window = [plane.indirect(offsets[:, h * HALF // 16 : (h + 1) * HALF // 16]) for h in range(2)]
             in_place = g == 1 and j >= 2
             nc.vector.tensor_copy(picked[g, 0][:, :, j] if in_place else gathered[g, 0][:, j, :], window[0])
             nc.scalar.activation(gathered[g, 1][:, j, :], window[1], COPY)

@@ -34,7 +34,7 @@ LATE_SLOT = 2
 W_HALF = H // 2
 M_HALF = W_HALF // PACK
 M_VECTOR = (40, 56)
-M_VECTOR_FIRST = 80
+M_VECTOR_FIRST = 64
 M_AHEAD = 36
 
 
@@ -55,19 +55,15 @@ def tile_picked_dconv_silu_e_kernel(tc, xT, w1, w2_words, w2_scales, taps, offs,
         nc.gpsimd.memset(w2_plane[:], 0)
         middle = keep.tile([P, 2, HALF], F32, name="middle")
         nc.gpsimd.memset(middle[:, 0, 0:1], 0.0)
-        planes = {}
-
-        def load_plane(g, j):
-            rows = xT[g * K_PASS : (g + 1) * K_PASS, :].rearrange("(p j) t -> p j t", j=PACK)
-            planes[g, j] = keep.tile([P, T], F32, name=f"plane{g}{j}", tag=f"plane{g}{j}", align_bytes=64)
-            nc.sync.dma_start(out=planes[g, j][:], in_=rows[:, j, :])
-
-        nc.sync.dma_start(out=w_first[:], in_=w1[0:K_PASS, :].rearrange("(p j) c -> p j c", j=PACK))
-        nc.sync.dma_start(offsets[:], offs)
         first_x = keep.tile([P, PACK, T], F32, name="first_x", align_bytes=64)
-        nc.sync.dma_start(out=first_x[:], in_=xT[0:K_PASS, :].rearrange("(p j) t -> p j t", j=PACK))
-        for j in range(PACK):
-            load_plane(1, j)
+        second_x = keep.tile([P, PACK - 1, T], F32, name="second_x", align_bytes=64)
+        last_x = keep.tile([P, T], F32, name="last_x", tag="last_x", align_bytes=64)
+        rows = xT.rearrange("(g p j) t -> g p j t", g=2, j=PACK)
+        nc.sync.dma_start(out=first_x[:], in_=rows[0])
+        nc.sync.dma_start(offsets[:], offs)
+        nc.sync.dma_start(out=second_x[:], in_=rows[1, :, : PACK - 1, :])
+        nc.sync.dma_start(out=w_first[:], in_=w1[0:K_PASS, :].rearrange("(p j) c -> p j c", j=PACK))
+        nc.sync.dma_start(out=last_x[:], in_=rows[1, :, PACK - 1, :])
         run = w1[K_PASS:K, :].rearrange("(p j) c -> p (j c)", j=PACK)
         for cut in (slice(0, PACK * H - W_HALF), slice(PACK * H - W_HALF, PACK * H)):
             nc.sync.dma_start(out=w_last[:].rearrange("p j c -> p (j c)")[:, cut], in_=run[:, cut])
@@ -81,7 +77,7 @@ def tile_picked_dconv_silu_e_kernel(tc, xT, w1, w2_words, w2_scales, taps, offs,
         acc = keep.tile([P, PACK, S + 8], F32, name="acc")
         nc.scalar.activation(acc[:, :, 0 : D - 1], zeros[:], SILU)
 
-        gathered = {(g, h): keep.tile([P, PACK, HALF], BF16 if g else F32, name=f"gathered{g}{h}", tag=f"gathered{g}{h}", align_bytes=64) for g in range(2) for h in range(2)}
+        gathered = {(g, h): keep.tile([P, PACK, HALF], F32, name=f"gathered{g}{h}", tag=f"gathered{g}{h}", align_bytes=64) for g in range(2) for h in range(2)}
         picked = {(g, h): keep.tile([P, HALF, PACK], BF16, name=f"picked{g}{h}", align_bytes=64) for g in range(2) for h in range(2)}
         x_codes = {}
         x_plane = {(g, h): keep.tile([P, HALF], U8, name=f"x_plane{g}{h}", align_bytes=64) for g in range(2) for h in range(2)}
@@ -91,7 +87,7 @@ def tile_picked_dconv_silu_e_kernel(tc, xT, w1, w2_words, w2_scales, taps, offs,
         hidden = [[psum.tile([P, HALF], F32, name=f"hidden{h}{t}", tag=f"bank{h}{t}") for t in range(PACK)] for h in range(2)]
 
         def gather(g, j):
-            plane = planes[g, j][:] if g else first_x[:, j, :]
+            plane = first_x[:, j, :] if g == 0 else last_x[:] if j == PACK - 1 else second_x[:, j, :]
             window = [plane.indirect(offsets[:, h * HALF // 16 : (h + 1) * HALF // 16]) for h in range(2)]
             in_place = g == 1 and j >= 2
             nc.vector.tensor_copy(picked[g, 0][:, :, j] if in_place else gathered[g, 0][:, j, :], window[0])
@@ -127,6 +123,16 @@ def tile_picked_dconv_silu_e_kernel(tc, xT, w1, w2_words, w2_scales, taps, offs,
                 x_codes[g, h].bitcast(FP8X4), x_plane[g, h][:], start=(g == 0), stop=(g == 1),
             )
 
+        for j in range(PACK):
+            gather(0, j)
+        for h in range(2):
+            weave(0, h, slice(0, PACK))
+        for h in range(2):
+            quantize_x(0, h, keep.tile([P, HALF], U32, name=f"x_codes0{h}", align_bytes=64)[:])
+        for j in range(PACK - 1):
+            gather(1, j)
+        for h in range(2):
+            weave(1, h, slice(0, 2))
         for pair in range(2):
             deal(nc.vector.tensor_copy, 0, pair, w_first, 0, M_VECTOR_FIRST, 0)
             deal(nc.scalar.copy, 0, pair, w_first, M_VECTOR_FIRST, P - M_VECTOR_FIRST, M_VECTOR_FIRST)
@@ -135,24 +141,12 @@ def tile_picked_dconv_silu_e_kernel(tc, xT, w1, w2_words, w2_scales, taps, offs,
             nc.vector.quantize_mx(
                 w_codes[0][:, cols].bitcast(FP8X4), w_plane[0][:, cols], dealt[0, pair][:].rearrange("p t m j -> p (t m j)")
             )
-        for j in range(PACK):
-            gather(0, j)
-        for h in range(2):
-            weave(0, h, slice(0, PACK))
-        for j in range(2):
-            gather(1, j)
-        for h in range(2):
-            weave(1, h, slice(0, 2))
-        gather(1, 2)
-        first_codes = keep.tile([P, 2, HALF], U32, name="first_codes", tag="plane12", align_bytes=64)
-        for h in range(2):
-            quantize_x(0, h, first_codes[:, h, :])
         for h in range(2):
             for t in range(PACK):
                 project(0, h, t)
         gather(1, PACK - 1)
         weave(1, 1, slice(2, PACK))
-        quantize_x(1, 0, keep.tile([P, HALF], U32, name="x_codes10", tag="plane13", align_bytes=64)[:])
+        quantize_x(1, 0, keep.tile([P, HALF], U32, name="x_codes10", tag="last_x", align_bytes=64)[:])
         quantize_x(1, 1, keep.tile([P, HALF], U32, name="x_codes11", align_bytes=64)[:])
         deal(nc.vector.tensor_copy, 1, 0, w_last, 0, M_AHEAD, 0)
         deal(nc.scalar.copy, 1, 0, w_last, M_AHEAD, M_HALF - M_AHEAD, M_AHEAD)

@@ -45,8 +45,8 @@ def tile_picked_dconv_silu_e_kernel(tc, xT, w1, w2_words, w2_scales, taps, offs,
         psum = ctx.enter_context(tc.psum_pool(name="psum", bufs=1))
 
         offsets = keep.tile([P, S // 16], U16, name="offsets")
-        w_first = keep.tile([P, PACK, H], F32, name="w_first")
-        w_last = keep.tile([P, PACK, H], F32, name="w_last", tag="w_last", align_bytes=64)
+        w_first = keep.tile([P, PACK, H], F32, name="w_first", align_bytes=256)
+        w_last = keep.tile([P, PACK, H], F32, name="w_last", align_bytes=256)
         tap = keep.tile([P, PACK, D], F32, name="tap")
         w2_codes = keep.tile([P, 2 * N], U8, name="w2_codes", align_bytes=64)
         w2_plane = keep.tile([P, N], U8, name="w2_plane", align_bytes=64)
@@ -55,9 +55,9 @@ def tile_picked_dconv_silu_e_kernel(tc, xT, w1, w2_words, w2_scales, taps, offs,
         nc.gpsimd.memset(w2_plane[:], 0)
         middle = keep.tile([P, 2, HALF], F32, name="middle")
         nc.gpsimd.memset(middle[:, 0, 0:1], 0.0)
-        first_x = keep.tile([P, PACK, T], F32, name="first_x", align_bytes=64)
-        second_x = keep.tile([P, PACK - 1, T], F32, name="second_x", align_bytes=64)
-        last_x = keep.tile([P, T], F32, name="last_x", tag="last_x", align_bytes=64)
+        first_x = keep.tile([P, PACK, T], F32, name="first_x", align_bytes=256)
+        second_x = keep.tile([P, PACK - 1, T], F32, name="second_x", align_bytes=256)
+        last_x = keep.tile([P, T], F32, name="last_x", tag="last_x", align_bytes=256)
         rows = xT.rearrange("(g p j) t -> g p j t", g=2, j=PACK)
         nc.sync.dma_start(out=first_x[:], in_=rows[0])
         nc.sync.dma_start(offsets[:], offs)
@@ -146,7 +146,7 @@ def tile_picked_dconv_silu_e_kernel(tc, xT, w1, w2_words, w2_scales, taps, offs,
                 project(0, h, t)
         gather(1, PACK - 1)
         weave(1, 1, slice(2, PACK))
-        quantize_x(1, 0, keep.tile([P, HALF], U32, name="x_codes10", tag="last_x", align_bytes=64)[:])
+        quantize_x(1, 0, keep.tile([P, HALF], U32, name="x_codes10", tag="last_x", align_bytes=256)[:])
         quantize_x(1, 1, keep.tile([P, HALF], U32, name="x_codes11", align_bytes=64)[:])
         deal(nc.vector.tensor_copy, 1, 0, w_last, 0, M_AHEAD, 0)
         deal(nc.scalar.copy, 1, 0, w_last, M_AHEAD, M_HALF - M_AHEAD, M_AHEAD)
@@ -237,7 +237,7 @@ def tile_picked_dconv_silu_e_kernel(tc, xT, w1, w2_words, w2_scales, taps, offs,
             finish(s, (0, 2, 1, 3) if s == HALF else (0, 3, 1, 2))
 
         products = [psum.tile([P, n], F32, name=f"product{c}", tag=f"bank0{c}") for c, (s, n) in enumerate(OUT_PIECES)]
-        results = {s: keep.tile([P, n], F32, name=f"result{s}") for s, n in STORES}
+        results = {s: keep.tile([P, n], F32, name=f"result{s}", align_bytes=256) for s, n in STORES}
         for c, (s, n) in enumerate(OUT_PIECES):
             for first in [first for first in pieces if s <= first < s + n]:
                 cols = slice(first - s, first - s + pieces[first])

@@ -33,9 +33,9 @@ ADDED_SLOT = 1
 LATE_SLOT = 2
 W_HALF = H // 2
 M_HALF = W_HALF // PACK
-M_VECTOR = (40, 56)
+M_VECTOR = (36, 40)
+M_AHEAD = 48
 M_VECTOR_FIRST = 64
-M_AHEAD = 36
 
 
 def tile_picked_dconv_silu_e_kernel(tc, xT, w1, w2_words, w2_scales, taps, offs, out):
@@ -64,9 +64,9 @@ def tile_picked_dconv_silu_e_kernel(tc, xT, w1, w2_words, w2_scales, taps, offs,
         nc.sync.dma_start(out=second_x[:], in_=rows[1, :, : PACK - 1, :])
         nc.sync.dma_start(out=w_first[:], in_=w1[0:K_PASS, :].rearrange("(p j) c -> p j c", j=PACK))
         nc.sync.dma_start(out=last_x[:], in_=rows[1, :, PACK - 1, :])
-        run = w1[K_PASS:K, :].rearrange("(p j) c -> p (j c)", j=PACK)
-        for cut in (slice(0, PACK * H - W_HALF), slice(PACK * H - W_HALF, PACK * H)):
-            nc.sync.dma_start(out=w_last[:].rearrange("p j c -> p (j c)")[:, cut], in_=run[:, cut])
+        for half in range(2):
+            cols = slice(half * W_HALF, (half + 1) * W_HALF)
+            nc.sync.dma_start(out=w_last[:, :, cols], in_=w1[K_PASS:K, cols].rearrange("(p j) c -> p j c", j=PACK))
         nc.sync.dma_start(out=tap[:], in_=taps.rearrange("(p t) d -> p t d", t=PACK))
         nc.sync.dma_start(out=w2_codes[:].bitcast(I32), in_=w2_words[0].bitcast(I32))
         for q in range(4):
@@ -148,16 +148,16 @@ def tile_picked_dconv_silu_e_kernel(tc, xT, w1, w2_words, w2_scales, taps, offs,
         weave(1, 1, slice(2, PACK))
         quantize_x(1, 0, keep.tile([P, HALF], U32, name="x_codes10", tag="last_x", align_bytes=256)[:])
         quantize_x(1, 1, keep.tile([P, HALF], U32, name="x_codes11", align_bytes=64)[:])
-        deal(nc.vector.tensor_copy, 1, 0, w_last, 0, M_AHEAD, 0)
-        deal(nc.scalar.copy, 1, 0, w_last, M_AHEAD, M_HALF - M_AHEAD, M_AHEAD)
-        cut = M_HALF + M_VECTOR[0]
-        deal(nc.vector.tensor_copy, 1, 0, w_last, M_HALF, M_VECTOR[0], M_HALF)
-        deal(nc.scalar.copy, 1, 0, w_last, cut, P - cut, cut)
-        cut = P - M_VECTOR[1]
-        deal(nc.scalar.copy, 1, 1, w_last, 0, cut, 0)
-        deal(nc.vector.tensor_copy, 1, 1, w_last, cut, M_VECTOR[1], cut)
+        deal(nc.scalar.copy, 1, 0, w_last, 0, M_HALF, 0)
+        deal(nc.scalar.copy, 1, 1, w_last, 0, M_AHEAD, 0)
         for t in range(2):
-            quantize_w_last(t, 0, P)
+            quantize_w_last(t, 0, M_HALF)
+        for pair, first in enumerate((M_HALF, M_AHEAD)):
+            cut = first + M_VECTOR[pair]
+            deal(nc.vector.tensor_copy, 1, pair, w_last, first, M_VECTOR[pair], first)
+            deal(nc.scalar.copy, 1, pair, w_last, cut, P - cut, cut)
+        for t in range(2):
+            quantize_w_last(t, M_HALF, M_HALF)
         nc.vector.quantize_mx(
             w_codes[1][:, 2 * P :].bitcast(FP8X4), w_plane[1][:, 2 * P :], dealt[1, 1][:].rearrange("p t m j -> p (t m j)")
         )

@@ -23,8 +23,8 @@ PACK = 4
 K_PASS = P * PACK
 HALF = S // 2
 ACT_PIECES = ((0, 128), (128, 128), (256, 128), (384, 64), (448, 64))
-OUT_PIECES = ((0, 128), (128, 128), (256, 128), (384, 128))
-STORES = ((0, 256), (256, 128), (384, 128))
+OUT_PIECES = ((0, 128), (128, 128), (256, 128), (384, 64), (448, 64))
+STORES = ((0, 256), (256, 192), (448, 64))
 GPSIMD_SLOTS = (0,)
 SECOND_ORDER = (0, 1, 2, 3)
 BANK_ORDER = ((0, 0), (0, 1), (1, 0), (0, 2), (0, 3), (1, 1), (1, 2), (1, 3))
@@ -191,8 +191,8 @@ def tile_picked_dconv_silu_e_kernel(tc, xT, w1, w2_words, w2_scales, taps, offs,
         pieces = dict(ACT_PIECES)
         summed = {s: keep.tile([P, n // PACK, PACK, PACK], F32, name=f"summed{s}") for s, n in ACT_PIECES}
         z = {s: keep.tile([P, n, PACK], BF16, name=f"z{s}", align_bytes=64) for s, n in ACT_PIECES}
-        z_codes = [keep.tile([P, n], U32, name=f"z_codes{s}", align_bytes=64) for s, n in OUT_PIECES]
-        z_plane = [keep.tile([P, n], U8, name=f"z_plane{s}", align_bytes=64) for s, n in OUT_PIECES]
+        z_codes = keep.tile([P, S], U32, name="z_codes", align_bytes=64)
+        z_plane = keep.tile([P, S], U8, name="z_plane", align_bytes=64)
 
         def add_tap1(h, t):
             n = HALF - 1 if h == 1 or t in GPSIMD_SLOTS else HALF
@@ -236,18 +236,17 @@ def tile_picked_dconv_silu_e_kernel(tc, xT, w1, w2_words, w2_scales, taps, offs,
         for s in (HALF, 384, 448):
             finish(s, (0, 2, 1, 3) if s == HALF else (0, 3, 1, 2))
 
-        products = [psum.tile([P, n], F32, name=f"product{c}", tag=f"bank0{c}") for c, (s, n) in enumerate(OUT_PIECES)]
+        products = [psum.tile([P, P], F32, name=f"product{c}", tag=f"bank{c // PACK}{c % PACK}") for c in range(len(OUT_PIECES))]
         results = {s: keep.tile([P, n], F32, name=f"result{s}", align_bytes=256) for s, n in STORES}
         for c, (s, n) in enumerate(OUT_PIECES):
-            for first in [first for first in pieces if s <= first < s + n]:
-                cols = slice(first - s, first - s + pieces[first])
-                nc.vector.quantize_mx(z_codes[c][:, cols].bitcast(FP8X4), z_plane[c][:, cols], z[first][:].rearrange("p s t -> p (s t)"))
+            nc.vector.quantize_mx(z_codes[:, s : s + n].bitcast(FP8X4), z_plane[:, s : s + n], z[s][:].rearrange("p s t -> p (s t)"))
+            cols = slice(s + n - P, s + n)
             nc.tensor.matmul_mx(
-                products[c][:], w2_codes[:].bitcast(FP4X4), w2_plane[:], z_codes[c][:].bitcast(FP8X4), z_plane[c][:],
+                products[c][:], w2_codes[:].bitcast(FP4X4), w2_plane[:], z_codes[:, cols].bitcast(FP8X4), z_plane[:, cols],
                 start=True, stop=True,
             )
         for first, width in STORES:
             for c, (s, n) in enumerate(OUT_PIECES):
                 if first <= s < first + width:
-                    nc.scalar.copy(results[first][:, s - first : s - first + n], products[c][:])
+                    nc.scalar.copy(results[first][:, s - first : s - first + n], products[c][:, P - n :])
             nc.sync.dma_start(out=out[:, first : first + width], in_=results[first][:])

@@ -35,7 +35,7 @@ W_HALF = H // 2
 M_HALF = W_HALF // PACK
 M_VECTOR = (36, 40)
 M_AHEAD = 48
-M_VECTOR_FIRST = 64
+M_VECTOR_FIRST = 72
 
 
 def tile_picked_dconv_silu_e_kernel(tc, xT, w1, w2_words, w2_scales, taps, offs, out):
@@ -90,7 +90,10 @@ def tile_picked_dconv_silu_e_kernel(tc, xT, w1, w2_words, w2_scales, taps, offs,
             plane = first_x[:, j, :] if g == 0 else last_x[:] if j == PACK - 1 else second_x[:, j, :]
             window = [plane.indirect(offsets[:, h * HALF // 16 : (h + 1) * HALF // 16]) for h in range(2)]
             in_place = g == 1 and j >= 2
-            nc.vector.tensor_copy(picked[g, 0][:, :, j] if in_place else gathered[g, 0][:, j, :], window[0])
+            if (g, j) == (1, 0):
+                nc.scalar.activation(gathered[g, 0][:, j, :], window[0], COPY)
+            else:
+                nc.vector.tensor_copy(picked[g, 0][:, :, j] if in_place else gathered[g, 0][:, j, :], window[0])
             nc.scalar.activation(gathered[g, 1][:, j, :], window[1], COPY)
 
         def weave(g, h, rows):

@@ -53,8 +53,8 @@ def tile_picked_dconv_silu_e_kernel(tc, xT, w1, w2_words, w2_scales, taps, offs,
         zeros = keep.tile([P, PACK, D - 1], F32, name="zeros")
         nc.gpsimd.memset(zeros[:], 0.0)
         nc.gpsimd.memset(w2_plane[:], 0)
-        middle = keep.tile([P, 2, HALF], F32, name="middle")
-        nc.gpsimd.memset(middle[:, 0, 0:1], 0.0)
+        middle = keep.tile([P, 3, HALF], F32, name="middle")
+        nc.gpsimd.memset(middle[:, 1, 0:1], 0.0)
         first_x = keep.tile([P, PACK, T], F32, name="first_x", align_bytes=256)
         second_x = keep.tile([P, PACK - 1, T], F32, name="second_x", align_bytes=256)
         last_x = keep.tile([P, T], F32, name="last_x", tag="last_x", align_bytes=256)
@@ -168,18 +168,15 @@ def tile_picked_dconv_silu_e_kernel(tc, xT, w1, w2_words, w2_scales, taps, offs,
             project(1, h, t)
 
         plain = {t: keep.tile([P, HALF + 8], F32, name=f"plain{t}") for t in GPSIMD_SLOTS}
-        older = {t: keep.tile([P, HALF], F32, name=f"older{t}")[:] for t in GPSIMD_SLOTS}
-        added = keep.tile([P, 2, HALF], F32, name="added")
-        older[ADDED_SLOT], older[LATE_SLOT] = added[:, 0, :], added[:, 1, :]
+        added = keep.tile([P, 3, HALF], F32, name="added")
+        older = {t: added[:, t, :] for t in range(3)}
         for h, t in BANK_ORDER:
             n = HALF - 2 if h == 1 or t in GPSIMD_SLOTS else HALF
             first = h * HALF + 2
             if h == 1 and t in GPSIMD_SLOTS:
-                scaled = keep.tile([P, HALF], F32, name=f"scaled{t}")
                 nc.scalar.copy(plain[t][:, 2 : HALF + 1], hidden[1][t][:, : HALF - 1])
-                nc.gpsimd.tensor_scalar(older[t], plain[t][:, 0:HALF], tap[:, t, 2:3], 0.0, MULT, ADD)
-                nc.gpsimd.tensor_scalar(scaled[:], plain[t][:, 1 : HALF + 1], tap[:, t, 1:2], 0.0, MULT, ADD)
-                nc.gpsimd.tensor_tensor(older[t], older[t], scaled[:], ADD)
+                nc.gpsimd.tensor_scalar(acc[:, t, HALF:S], plain[t][:, 0:HALF], tap[:, t, 2:3], 0.0, MULT, ADD)
+                nc.gpsimd.tensor_scalar(middle[:, t, :], plain[t][:, 1 : HALF + 1], tap[:, t, 1:2], 0.0, MULT, ADD)
             elif (h, t) == VECTOR_BANK:
                 nc.vector.tensor_scalar(acc[:, t, first : first + n], hidden[h][t][:, :n], tap[:, t, 2:3], None, MULT)
             else:
@@ -187,9 +184,9 @@ def tile_picked_dconv_silu_e_kernel(tc, xT, w1, w2_words, w2_scales, taps, offs,
                 if t in GPSIMD_SLOTS:
                     nc.scalar.copy(plain[t][:, 0:2], hidden[0][t][:, n:])
                 if (h, t) == (1, ADDED_SLOT):
-                    nc.scalar.activation(middle[:, 0, 1:], hidden[h][t][:, : HALF - 1], COPY, scale=tap[:, t, 1:2])
+                    nc.scalar.activation(middle[:, 1, 1:], hidden[h][t][:, : HALF - 1], COPY, scale=tap[:, t, 1:2])
                 if (h, t) == (1, LATE_SLOT):
-                    nc.scalar.activation(middle[:, 1, P:], hidden[h][t][:, P - 1 : HALF - 1], COPY, scale=tap[:, t, 1:2])
+                    nc.scalar.activation(middle[:, 2, P:], hidden[h][t][:, P - 1 : HALF - 1], COPY, scale=tap[:, t, 1:2])
 
         pieces = dict(ACT_PIECES)
         summed = {s: keep.tile([P, n // PACK, PACK, PACK], F32, name=f"summed{s}") for s, n in ACT_PIECES}
@@ -227,8 +224,8 @@ def tile_picked_dconv_silu_e_kernel(tc, xT, w1, w2_words, w2_scales, taps, offs,
             add_tap0(0, t - 1)
         add_tap0(0, PACK - 1)
         activate(0)
-        for slots, cols in ((1, slice(0, P)), (2, slice(P, 192)), (2, slice(192, HALF))):
-            own = acc[:, ADDED_SLOT : ADDED_SLOT + slots, HALF + cols.start : HALF + cols.stop]
+        for slots, cols in ((2, slice(0, P)), (3, slice(P, HALF))):
+            own = acc[:, :slots, HALF + cols.start : HALF + cols.stop]
             nc.gpsimd.tensor_tensor(added[:, :slots, cols], own, middle[:, :slots, cols], ADD)
         finish(P, range(PACK))
         window = acc[:, LATE_SLOT, HALF + 1 : HALF + P]
@@ -237,7 +234,7 @@ def tile_picked_dconv_silu_e_kernel(tc, xT, w1, w2_words, w2_scales, taps, offs,
             if t not in older:
                 add_tap1(1, t)
         for s in (HALF, 384, 448):
-            finish(s, (0, 2, 1, 3) if s == HALF else (0, 3, 1, 2))
+            finish(s, (0, 1, 2, 3) if s == HALF else (3, 0, 1, 2))
 
         products = [psum.tile([P, P], F32, name=f"product{c}", tag=f"bank{c // PACK}{c % PACK}") for c in range(len(OUT_PIECES))]
         results = {s: keep.tile([P, n], F32, name=f"result{s}", align_bytes=256) for s, n in STORES}

@@ -35,6 +35,7 @@ W_HALF = H // 2
 M_HALF = W_HALF // PACK
 M_VECTOR = (36, 40)
 M_AHEAD = 48
+ACC_SHIFT = 6
 M_VECTOR_FIRST = 72
 
 
@@ -44,17 +45,17 @@ def tile_picked_dconv_silu_e_kernel(tc, xT, w1, w2_words, w2_scales, taps, offs,
         keep = ctx.enter_context(tc.tile_pool(name="keep", bufs=1))
         psum = ctx.enter_context(tc.psum_pool(name="psum", bufs=1))
 
-        offsets = keep.tile([P, S // 16], U16, name="offsets")
+        offsets = keep.tile([P, S // 16], U16, name="offsets", align_bytes=256)
         w_first = keep.tile([P, PACK, H], F32, name="w_first", align_bytes=256)
         w_last = keep.tile([P, PACK, H], F32, name="w_last", align_bytes=256)
-        tap = keep.tile([P, PACK, D], F32, name="tap")
-        w2_codes = keep.tile([P, 2 * N], U8, name="w2_codes", align_bytes=64)
-        w2_plane = keep.tile([P, N], U8, name="w2_plane", align_bytes=64)
+        tap = keep.tile([P, PACK, D], F32, name="tap", align_bytes=256)
+        w2_codes = keep.tile([P, 2 * N], U8, name="w2_codes", align_bytes=256)
+        w2_plane = keep.tile([P, N], U8, name="w2_plane", align_bytes=256)
         zeros = keep.tile([P, PACK, D - 1], F32, name="zeros")
         nc.gpsimd.memset(zeros[:], 0.0)
         nc.gpsimd.memset(w2_plane[:], 0)
         middle = keep.tile([P, 3, HALF], F32, name="middle")
-        nc.gpsimd.memset(middle[:, 1, 0:1], 0.0)
+        nc.gpsimd.memset(middle[:, 0:2, 0:1], 0.0)
         first_x = keep.tile([P, PACK, T], F32, name="first_x", align_bytes=256)
         second_x = keep.tile([P, PACK - 1, T], F32, name="second_x", align_bytes=256)
         last_x = keep.tile([P, T], F32, name="last_x", tag="last_x", align_bytes=256)
@@ -74,7 +75,7 @@ def tile_picked_dconv_silu_e_kernel(tc, xT, w1, w2_words, w2_scales, taps, offs,
                 out=w2_plane[32 * q : 32 * q + 4, :].bitcast(I32), in_=w2_scales[0, 4 * q : 4 * q + 4, :].bitcast(I32)
             )
 
-        acc = keep.tile([P, PACK, S + 8], F32, name="acc")
+        acc = keep.tile([P, PACK, S + 8], F32, name="acc")[:, :, ACC_SHIFT : ACC_SHIFT + S]
         nc.scalar.activation(acc[:, :, 0 : D - 1], zeros[:], SILU)
 
         gathered = {(g, h): keep.tile([P, PACK, HALF], F32, name=f"gathered{g}{h}", tag=f"gathered{g}{h}", align_bytes=64) for g in range(2) for h in range(2)}
@@ -171,18 +172,16 @@ def tile_picked_dconv_silu_e_kernel(tc, xT, w1, w2_words, w2_scales, taps, offs,
         added = keep.tile([P, 3, HALF], F32, name="added")
         older = {t: added[:, t, :] for t in range(3)}
         for h, t in BANK_ORDER:
-            n = HALF - 2 if h == 1 or t in GPSIMD_SLOTS else HALF
+            n = HALF - 2 if h == 1 else HALF
             first = h * HALF + 2
             if h == 1 and t in GPSIMD_SLOTS:
-                nc.scalar.copy(plain[t][:, 2 : HALF + 1], hidden[1][t][:, : HALF - 1])
-                nc.gpsimd.tensor_scalar(acc[:, t, HALF:S], plain[t][:, 0:HALF], tap[:, t, 2:3], 0.0, MULT, ADD)
-                nc.gpsimd.tensor_scalar(middle[:, t, :], plain[t][:, 1 : HALF + 1], tap[:, t, 1:2], 0.0, MULT, ADD)
+                nc.scalar.copy(plain[t][:, : HALF - 1], hidden[1][t][:, : HALF - 1])
+                nc.gpsimd.tensor_scalar(acc[:, t, first : first + n], plain[t][:, :n], tap[:, t, 2:3], 0.0, MULT, ADD)
+                nc.gpsimd.tensor_scalar(middle[:, t, 1:], plain[t][:, : HALF - 1], tap[:, t, 1:2], 0.0, MULT, ADD)
             elif (h, t) == VECTOR_BANK:
                 nc.vector.tensor_scalar(acc[:, t, first : first + n], hidden[h][t][:, :n], tap[:, t, 2:3], None, MULT)
             else:
                 nc.scalar.activation(acc[:, t, first : first + n], hidden[h][t][:, :n], COPY, scale=tap[:, t, 2:3])
-                if t in GPSIMD_SLOTS:
-                    nc.scalar.copy(plain[t][:, 0:2], hidden[0][t][:, n:])
                 if (h, t) == (1, ADDED_SLOT):
                     nc.scalar.activation(middle[:, 1, 1:], hidden[h][t][:, : HALF - 1], COPY, scale=tap[:, t, 1:2])
                 if (h, t) == (1, LATE_SLOT):
@@ -195,7 +194,7 @@ def tile_picked_dconv_silu_e_kernel(tc, xT, w1, w2_words, w2_scales, taps, offs,
         z_plane = keep.tile([P, S], U8, name="z_plane", align_bytes=64)
 
         def add_tap1(h, t):
-            n = HALF - 1 if h == 1 or t in GPSIMD_SLOTS else HALF
+            n = HALF - 1 if h == 1 else HALF
             window = acc[:, t, h * HALF + 1 : h * HALF + n + 1]
             nc.vector.scalar_tensor_tensor(window, hidden[h][t][:, :n], tap[:, t, 1:2], window, MULT, ADD)
 

from contextlib import ExitStack

import concourse.mybir as mybir

K, T, S, D, H, N = 1024, 2048, 512, 3, 512, 128
FLOPS = 2 * K * H * S + 2 * H * N * S

F32 = mybir.dt.float32
BF16 = mybir.dt.bfloat16
I32 = mybir.dt.int32
U32 = mybir.dt.uint32
U16 = mybir.dt.uint16
U8 = mybir.dt.uint8
FP8X4 = mybir.dt.float8_e4m3fn_x4
FP4X4 = mybir.dt.float4_e2m1fn_x4
MULT = mybir.AluOpType.mult
ADD = mybir.AluOpType.add
COPY = mybir.ActivationFunctionType.Copy
SILU = mybir.ActivationFunctionType.Silu

P = 128
PACK = 4
K_PASS = P * PACK
HALF = S // 2
ACT_PIECES = ((0, 128), (128, 128), (256, 128), (384, 64), (448, 64))
OUT_PIECES = ((0, 128), (128, 128), (256, 128), (384, 64), (448, 64))
STORES = ((0, 256), (256, 192), (448, 64))
GPSIMD_SLOTS = (0,)
SECOND_ORDER = (0, 1, 2, 3)
BANK_ORDER = ((0, 0), (0, 1), (1, 0), (0, 2), (0, 3), (1, 1), (1, 2), (1, 3))
VECTOR_BANK = (0, 1)
ADDED_SLOT = 1
LATE_SLOT = 2
W_HALF = H // 2
M_HALF = W_HALF // PACK
M_VECTOR = (36, 40)
M_AHEAD = 48
ACC_SHIFT = 6
M_VECTOR_FIRST = 72


def tile_picked_dconv_silu_e_kernel(tc, xT, w1, w2_words, w2_scales, taps, offs, out):
    nc = tc.nc
    with ExitStack() as ctx:
        keep = ctx.enter_context(tc.tile_pool(name="keep", bufs=1))
        psum = ctx.enter_context(tc.psum_pool(name="psum", bufs=1))

        offsets = keep.tile([P, S // 16], U16, name="offsets", align_bytes=256)
        w_first = keep.tile([P, PACK, H], F32, name="w_first", align_bytes=256)
        w_last = keep.tile([P, PACK, H], F32, name="w_last", align_bytes=256)
        tap = keep.tile([P, PACK, D], F32, name="tap", align_bytes=256)
        w2_codes = keep.tile([P, 2 * N], U8, name="w2_codes", align_bytes=256)
        w2_plane = keep.tile([P, N], U8, name="w2_plane", align_bytes=256)
        zeros = keep.tile([P, PACK, D - 1], F32, name="zeros")
        nc.gpsimd.memset(zeros[:], 0.0)
        nc.gpsimd.memset(w2_plane[:], 0)
        middle = keep.tile([P, 3, HALF], F32, name="middle")
        nc.gpsimd.memset(middle[:, 0:2, 0:1], 0.0)
        first_x = keep.tile([P, PACK, T], F32, name="first_x", align_bytes=256)
        second_x = keep.tile([P, PACK - 1, T], F32, name="second_x", align_bytes=256)
        last_x = keep.tile([P, T], F32, name="last_x", tag="last_x", align_bytes=256)
        rows = xT.rearrange("(g p j) t -> g p j t", g=2, j=PACK)
        nc.sync.dma_start(out=first_x[:], in_=rows[0])
        nc.sync.dma_start(offsets[:], offs)
        nc.sync.dma_start(out=second_x[:], in_=rows[1, :, : PACK - 1, :])
        nc.sync.dma_start(out=w_first[:], in_=w1[0:K_PASS, :].rearrange("(p j) c -> p j c", j=PACK))
        nc.sync.dma_start(out=last_x[:], in_=rows[1, :, PACK - 1, :])
        for half in range(2):
            cols = slice(half * W_HALF, (half + 1) * W_HALF)
            nc.sync.dma_start(out=w_last[:, :, cols], in_=w1[K_PASS:K, cols].rearrange("(p j) c -> p j c", j=PACK))
        nc.sync.dma_start(out=tap[:], in_=taps.rearrange("(p t) d -> p t d", t=PACK))
        nc.sync.dma_start(out=w2_codes[:].bitcast(I32), in_=w2_words[0].bitcast(I32))
        for q in range(4):
            nc.sync.dma_start(
                out=w2_plane[32 * q : 32 * q + 4, :].bitcast(I32), in_=w2_scales[0, 4 * q : 4 * q + 4, :].bitcast(I32)
            )

        acc = keep.tile([P, PACK, S + 8], F32, name="acc")[:, :, ACC_SHIFT : ACC_SHIFT + S]
        nc.scalar.activation(acc[:, :, 0 : D - 1], zeros[:], SILU)

        gathered = {(g, h): keep.tile([P, PACK, HALF], F32, name=f"gathered{g}{h}", tag=f"gathered{g}{h}", align_bytes=64) for g in range(2) for h in range(2)}
        picked = {(g, h): keep.tile([P, HALF, PACK], BF16, name=f"picked{g}{h}", align_bytes=64) for g in range(2) for h in range(2)}
        x_codes = {}
        x_plane = {(g, h): keep.tile([P, HALF], U8, name=f"x_plane{g}{h}", align_bytes=64) for g in range(2) for h in range(2)}
        dealt = {(g, pair): keep.tile([P, 2, P, PACK], BF16, name=f"dealt{g}{pair}", align_bytes=64) for g in range(2) for pair in range(2)}
        w_codes = [keep.tile([P, H], U32, name=f"w_codes{g}", align_bytes=64) for g in range(2)]
        w_plane = [keep.tile([P, H], U8, name=f"w_plane{g}", align_bytes=64) for g in range(2)]
        hidden = [[psum.tile([P, HALF], F32, name=f"hidden{h}{t}", tag=f"bank{h}{t}") for t in range(PACK)] for h in range(2)]

        def gather(g, j):
            plane = first_x[:, j, :] if g == 0 else last_x[:] if j == PACK - 1 else second_x[:, j, :]
            window = [plane.indirect(offsets[:, h * HALF // 16 : (h + 1) * HALF // 16]) for h in range(2)]
            in_place = g == 1 and j >= 2
            if (g, j) == (1, 0):
                nc.scalar.activation(gathered[g, 0][:, j, :], window[0], COPY)
            else:
                nc.vector.tensor_copy(picked[g, 0][:, :, j] if in_place else gathered[g, 0][:, j, :], window[0])
            nc.scalar.activation(gathered[g, 1][:, j, :], window[1], COPY)

        def weave(g, h, rows):
            nc.vector.tensor_copy(
                picked[g, h][:, :, rows].rearrange("p (s i) j -> p s j i", i=2),
                gathered[g, h][:, rows, :].rearrange("p j (s i) -> p s j i", i=2),
            )

        def quantize_x(g, h, codes):
            x_codes[g, h] = codes
            nc.vector.quantize_mx(
                codes.bitcast(FP8X4), x_plane[g, h][:],
                picked[g, h][:].rearrange("p s j -> p (s j)"),
            )

        def deal(copy, g, pair, raw, m_raw, m_count, m_dealt):
            src = raw[:].rearrange("p j (m t) -> p m j t", t=PACK)[:, m_raw : m_raw + m_count, :, 2 * pair : 2 * pair + 2]
            dst = dealt[g, pair][:].rearrange("p t m j -> p m j t")[:, m_dealt : m_dealt + m_count, :, :]
            copy(dst, src)

        def quantize_w_last(t, m, count):
            cols = slice(t * P + m, t * P + m + count)
            values = dealt[1, t // 2][:, t % 2, m : m + count].rearrange("p m j -> p (m j)")
            nc.vector.quantize_mx(w_codes[1][:, cols].bitcast(FP8X4), w_plane[1][:, cols], values)

        def project(g, h, t):
            cols = slice(t * P, (t + 1) * P)
            nc.tensor.matmul_mx(
                hidden[h][t][:], w_codes[g][:, cols].bitcast(FP8X4), w_plane[g][:, cols],
                x_codes[g, h].bitcast(FP8X4), x_plane[g, h][:], start=(g == 0), stop=(g == 1),
            )

        for j in range(PACK):
            gather(0, j)
        for h in range(2):
            weave(0, h, slice(0, PACK))
        for h in range(2):
            quantize_x(0, h, keep.tile([P, HALF], U32, name=f"x_codes0{h}", align_bytes=64)[:])
        for j in range(PACK - 1):
            gather(1, j)
        for h in range(2):
            weave(1, h, slice(0, 2))
        for pair in range(2):
            deal(nc.vector.tensor_copy, 0, pair, w_first, 0, M_VECTOR_FIRST, 0)
            deal(nc.scalar.copy, 0, pair, w_first, M_VECTOR_FIRST, P - M_VECTOR_FIRST, M_VECTOR_FIRST)
        for pair in range(2):
            cols = slice(pair * 2 * P, (pair + 1) * 2 * P)
            nc.vector.quantize_mx(
                w_codes[0][:, cols].bitcast(FP8X4), w_plane[0][:, cols], dealt[0, pair][:].rearrange("p t m j -> p (t m j)")
            )
        for h in range(2):
            for t in range(PACK):
                project(0, h, t)
        gather(1, PACK - 1)
        weave(1, 1, slice(2, PACK))
        quantize_x(1, 0, keep.tile([P, HALF], U32, name="x_codes10", tag="last_x", align_bytes=256)[:])
        quantize_x(1, 1, keep.tile([P, HALF], U32, name="x_codes11", align_bytes=64)[:])
        deal(nc.scalar.copy, 1, 0, w_last, 0, M_HALF, 0)
        deal(nc.scalar.copy, 1, 1, w_last, 0, M_AHEAD, 0)
        for t in range(2):
            quantize_w_last(t, 0, M_HALF)
        for pair, first in enumerate((M_HALF, M_AHEAD)):
            cut = first + M_VECTOR[pair]
            deal(nc.vector.tensor_copy, 1, pair, w_last, first, M_VECTOR[pair], first)
            deal(nc.scalar.copy, 1, pair, w_last, cut, P - cut, cut)
        for t in range(2):
            quantize_w_last(t, M_HALF, M_HALF)
        nc.vector.quantize_mx(
            w_codes[1][:, 2 * P :].bitcast(FP8X4), w_plane[1][:, 2 * P :], dealt[1, 1][:].rearrange("p t m j -> p (t m j)")
        )
        for h, t in BANK_ORDER:
            project(1, h, t)

        plain = {t: keep.tile([P, HALF + 8], F32, name=f"plain{t}") for t in GPSIMD_SLOTS}
        added = keep.tile([P, 3, HALF], F32, name="added")
        older = {t: added[:, t, :] for t in range(3)}
        for h, t in BANK_ORDER:
            n = HALF - 2 if h == 1 else HALF
            first = h * HALF + 2
            if h == 1 and t in GPSIMD_SLOTS:
                nc.scalar.copy(plain[t][:, : HALF - 1], hidden[1][t][:, : HALF - 1])
                nc.gpsimd.tensor_scalar(acc[:, t, first : first + n], plain[t][:, :n], tap[:, t, 2:3], 0.0, MULT, ADD)
                nc.gpsimd.tensor_scalar(middle[:, t, 1:], plain[t][:, : HALF - 1], tap[:, t, 1:2], 0.0, MULT, ADD)
            elif (h, t) == VECTOR_BANK:
                nc.vector.tensor_scalar(acc[:, t, first : first + n], hidden[h][t][:, :n], tap[:, t, 2:3], None, MULT)
            else:
                nc.scalar.activation(acc[:, t, first : first + n], hidden[h][t][:, :n], COPY, scale=tap[:, t, 2:3])
                if (h, t) == (1, ADDED_SLOT):
                    nc.scalar.activation(middle[:, 1, 1:], hidden[h][t][:, : HALF - 1], COPY, scale=tap[:, t, 1:2])
                if (h, t) == (1, LATE_SLOT):
                    nc.scalar.activation(middle[:, 2, P:], hidden[h][t][:, P - 1 : HALF - 1], COPY, scale=tap[:, t, 1:2])

        pieces = dict(ACT_PIECES)
        summed = {s: keep.tile([P, n // PACK, PACK, PACK], F32, name=f"summed{s}") for s, n in ACT_PIECES}
        z = {s: keep.tile([P, n, PACK], BF16, name=f"z{s}", align_bytes=64) for s, n in ACT_PIECES}
        z_codes = keep.tile([P, S], U32, name="z_codes", align_bytes=64)
        z_plane = keep.tile([P, S], U8, name="z_plane", align_bytes=64)

        def add_tap1(h, t):
            n = HALF - 1 if h == 1 else HALF
            window = acc[:, t, h * HALF + 1 : h * HALF + n + 1]
            nc.vector.scalar_tensor_tensor(window, hidden[h][t][:, :n], tap[:, t, 1:2], window, MULT, ADD)

        def add_tap0(s, t):
            n = pieces[s]
            bank = hidden[s // HALF][t][:, s % HALF : s % HALF + n]
            before = older[t][:, s - HALF : s - HALF + n] if t in older and s >= (HALF + P if t == LATE_SLOT else HALF) else acc[:, t, s : s + n]
            nc.vector.scalar_tensor_tensor(
                summed[s][:, :, t, :], bank.rearrange("p (s i) -> p s i", i=PACK), tap[:, t, 0:1],
                before.rearrange("p (s i) -> p s i", i=PACK), MULT, ADD,
            )

        def activate(s):
            nc.scalar.activation(
                z[s][:].rearrange("p (s i) t -> p s t i", i=PACK), summed[s][:], SILU
            )

        def finish(s, order):
            for t in order:
                add_tap0(s, t)
            activate(s)

        add_tap1(0, 0)
        for t in range(1, PACK):
            add_tap1(0, t)
            add_tap0(0, t - 1)
        add_tap0(0, PACK - 1)
        activate(0)
        for slots, cols in ((2, slice(0, P)), (3, slice(P, HALF))):
            own = acc[:, :slots, HALF + cols.start : HALF + cols.stop]
            nc.gpsimd.tensor_tensor(added[:, :slots, cols], own, middle[:, :slots, cols], ADD)
        finish(P, range(PACK))
        window = acc[:, LATE_SLOT, HALF + 1 : HALF + P]
        nc.vector.scalar_tensor_tensor(window, hidden[1][LATE_SLOT][:, : P - 1], tap[:, LATE_SLOT, 1:2], window, MULT, ADD)
        for t in range(PACK):
            if t not in older:
                add_tap1(1, t)
        for s in (HALF, 384, 448):
            finish(s, (0, 1, 2, 3) if s == HALF else (3, 0, 1, 2))

        products = [psum.tile([P, P], F32, name=f"product{c}", tag=f"bank{c // PACK}{c % PACK}") for c in range(len(OUT_PIECES))]
        results = {s: keep.tile([P, n], F32, name=f"result{s}", align_bytes=256) for s, n in STORES}
        for c, (s, n) in enumerate(OUT_PIECES):
            nc.vector.quantize_mx(z_codes[:, s : s + n].bitcast(FP8X4), z_plane[:, s : s + n], z[s][:].rearrange("p s t -> p (s t)"))
            cols = slice(s + n - P, s + n)
            nc.tensor.matmul_mx(
                products[c][:], w2_codes[:].bitcast(FP4X4), w2_plane[:], z_codes[:, cols].bitcast(FP8X4), z_plane[:, cols],
                start=True, stop=True,
            )
        for first, width in STORES:
            for c, (s, n) in enumerate(OUT_PIECES):
                if first <= s < first + width:
                    nc.scalar.copy(results[first][:, s - first : s - first + n], products[c][:, P - n :])
            nc.sync.dma_start(out=out[:, first : first + width], in_=results[first][:])
